import numpy as np, ml_dtypes
CORES = [40,64,80,88,96,104,120,144]
N = 8
import mx_ref
BF = ml_dtypes.bfloat16
def gentries(a):
    return np.ascontiguousarray(a.reshape(8, 16, -1).transpose(0, 2, 1)).reshape(8, -1)
def gtable(e):
    e = np.asarray(e); return np.ascontiguousarray(e.reshape(8, -1, 16).transpose(0, 2, 1)).reshape(128, -1).astype(np.int32)
def gcols(t, e):
    v = np.concatenate([t.reshape(8, 16, -1, 4), np.zeros((8, 16, 1, 4), BF)], axis=2)
    return np.ascontiguousarray(np.stack([v[g][:, e[g]] for g in range(8)])).reshape(128, -1)
def tile(rs):
    return np.stack(rs, axis=2).reshape(128, -1).astype(BF)
def cut(t, i, w=512):
    return t[:, w * i:w * i + w]
def pick(q, e):
    c = np.concatenate([q[0].reshape(128, -1, 4), np.zeros((128, 1, 4), np.uint8)], axis=1); s = np.concatenate([q[1], np.ones((16, 1), np.uint8)], axis=1)
    return (np.ascontiguousarray(c[:, e].reshape(128, -1)), np.ascontiguousarray(s[:, e]))
def join(*qs):
    return (np.concatenate([q[0] for q in qs], axis=1), np.concatenate([q[1] for q in qs], axis=1))
def put(q, e, v):
    c, s = q[0].reshape(128, -1, 4).copy(), q[1].copy(); c[:, e] = v[0].reshape(128, -1, 4); s[:, e] = v[1]
    return (c.reshape(128, -1), s)
def pk(c, s):
    return (np.ascontiguousarray(c), mx_ref.live(s))
def emit(q):
    return q[0], q[1]
def packed(v, rng):
    q = [mx_ref.quantize(np.ascontiguousarray(v[r])) for r in range(N)]
    return np.stack([a for a, b in q]), np.stack([mx_ref.plane(b, rng) for a, b in q])
def values_of_codes():
    e, c = np.zeros((128, 128, 4), np.float32), np.zeros((128, 2, 4), np.uint8)
    e[np.arange(128), np.arange(128), 0] = 1
    c[:127, :, 0] = np.arange(256).reshape(2, 128).T[:127]
    return mx_ref.matmul(mx_ref.quantize(e.reshape(128, 512).astype(BF)), (c.reshape(128, 8), np.full((16, 2), 127, np.uint8))).T.reshape(-1).astype(np.float64)
CODE_VALUE, SCALE_VALUE = values_of_codes(), 2.0 ** (np.arange(256) - 127.0)
def decode(q):
    return (CODE_VALUE[q[0]].reshape(16, 8, -1, 4) * SCALE_VALUE[q[1]][:, None, :, None] + 0.0).reshape(128, -1).astype(np.float32)
def f(rng, *shape):
    return mx_ref.flush((rng.standard_normal(shape, dtype=np.float32) * np.exp2(rng.integers(-2, 3, shape[:-1] + (1,)))).astype(BF))
def wide(rng, *shape, cols=0):
    v = rng.standard_normal(shape, dtype=np.float32) * np.exp2(rng.integers(-12, 13, shape)).astype(np.float32)
    if cols: v *= np.repeat(np.exp2(rng.integers(-cols, cols + 1, shape[:-2] + (1, shape[-1] // 4))) * (rng.random(shape[:-2] + (1, shape[-1] // 4)) > 0.0625), 4, axis=-1).astype(np.float32)
    return mx_ref.flush(v.astype(BF))
C, G, R, L = 384, 192, 3, 3
def big(v, k):
    v = v.astype(np.float32) * np.float32(k)
    v[np.abs(v) < np.float32(2.0 ** -16)] = 0
    return v.astype(BF)
def numbers_of(rng):
    return {"x": big(f(rng, N, 128, 4 * C), 1), "gh": big(f(rng, N, 128, 4 * G), 1), "u": np.array(f(rng, N, 128, 512)), "v": np.array(f(rng, N, 128, 512))}
def weights(rng, w):
    c, p = packed(np.stack([w] * N), rng)
    return {"wc": c, "ws": p}
def still(rng):
    w = np.zeros((128, 4, 128, 4), np.float32)
    i = np.arange(128)
    for b in range(4): w[i, b, i, b] = 32
    return weights(rng, w.reshape(128, 2048).astype(BF))
def matching(rng, n):
    p, i = np.arange(C), rng.permutation(C)[:n]
    h = n // 2
    p[i[:h]] = i[h:2 * h]
    p[i[h:2 * h]] = i[:h]
    return p
def stored(nx, pr):
    return {"nx": np.stack([gtable(nx[r]) for r in range(N)]), "pr": np.stack([gtable(pr[r].reshape(8, R * C)) for r in range(N)])}
def lists_of(rng, same=(), halves=()):
    nx = rng.permuted(np.tile(np.arange(C + G), (N, 8, 1)), axis=2)
    for r in same: nx[r] = nx[r, 0].copy()
    pr = np.stack([matching(rng, C) for i in range(N * 8 * R)]).reshape(N, 8, R, C)
    h = C // 2
    for r in halves:
        for g in range(8):
            for lo, hi in ((0, h), (h, C), (C, C + G)): nx[r, g, lo:hi] = lo + rng.permutation(hi - lo)
            i = h + rng.permutation(h)
            pr[r, g, 0, :h] = i
            pr[r, g, 0, i] = np.arange(h)
    return stored(nx, pr)
def signs(rng):
    return np.stack([rng.permutation(8) % 2 * 2.0 - 1.0 for r in range(N)])
def linked(rng, kind):
    i, a, b, n = rng.permutation(C + G), rng.permutation(C), C + rng.permutation(G), np.arange(C + G)
    if kind == 1: n[i] = np.roll(i, -1)
    if kind == 2:
        n[a] = np.roll(a, -1)
        n[b] = np.roll(b, -1)
    if kind == 3:
        i = np.concatenate([np.stack([a[:G], b], axis=1).reshape(-1), a[G:]])
        n[i] = np.roll(i, -1)
    if kind == 4:
        n[i[::2]] = i[1::2]
        n[i[1::2]] = i[::2]
    if kind == 5: n = np.roll(n, -1)
    if kind == 6: n = np.roll(n, 1)
    if kind == 7: n = i
    return n
def setup_inputs(rng):
    return {**numbers_of(rng), **lists_of(rng), **weights(rng, f(rng, 128, 2048))}
def setup_inputs_ties(rng):
    d = numbers_of(rng)
    c = big(f(rng, 128, 4), 1).astype(np.float32).reshape(8, 16, 4)[:, :8]
    k = np.stack([rng.permutation(C + G) % 2 for r in range(N)])
    k[rng.integers(N)] = 1
    a = np.where(k[:, None, None, :, None] == 1, c[None, :, :, None, :], np.float32(0.0)).astype(BF)
    d["x"].reshape(N, 8, 16, C, 4)[:, :, :8] = a[:, :, :, :C]
    d["gh"].reshape(N, 8, 16, G, 4)[:, :, :8] = a[:, :, :, C:]
    keep = np.zeros((8, 16, 8), bool)
    for g in range(8): keep[g, :8, g] = True
    u = d["u"].reshape(N, 8, 16, 128, 4)
    a = u[:, :, :, ::16].astype(np.float32)
    a[:, ~keep] = 0
    u[:, :, :, ::16] = a.astype(BF)
    w = np.array(f(rng, 128, 2048)).reshape(8, 16, 4, 8, 16, 4)
    w[:, 8:, :, :, :8] = 0
    for g in range(8):
        for h in range(8):
            if g != h: w[h, :, :, g, :8] = 0
    return {**d, **lists_of(rng), **weights(rng, w.reshape(128, 2048))}
def setup_inputs_near(rng):
    d = numbers_of(rng)
    m = np.stack([rng.permutation(8) + 1 for r in range(N)])
    s = rng.integers(0, 2 ** m[:, :, None], (N, 8, C + G))
    sg, o = signs(rng), rng.permutation(N)
    full = int(np.flatnonzero(o == 3)[0])
    h = 2 ** (m[full][:, None] - 1)
    s[full] = s[full] % h + h * ((np.arange(C + G) >= C // 2)[None, :] == (sg[full] > 0)[:, None])
    g = ((s[..., None] >> np.arange(8)) & 1) * np.exp2(np.arange(8) - 23.0)
    a = np.abs(np.concatenate([d["x"], d["gh"]], axis=2).astype(np.float32)).reshape(N, 8, 16, C + G, 4)
    a[:, :, 0] = 0
    a[:, :, 0, :, 0] = 0.5
    a[:, :, 8] = g[..., :4]
    a[:, :, 9] = g[..., 4:]
    a[:, :, 10:] = rng.integers(4, 8, (N, 8, 6, C + G, 4)) * 2.0 ** -20
    a = (a * np.float32(2.0 ** -7)).reshape(N, 128, 4 * (C + G)).astype(BF)
    k = sg * np.exp2(np.array([-30.0, 0.0, 24.0])[o % 3])[:, None]
    u = d["u"].reshape(N, 128, 128, 4)
    u[:, :, ::16] = 0
    for h in range(8):
        z = k[:, h].astype(np.float32).astype(BF)
        u[:, 16 * h, 16 * h, 0] = z
        u[:, 16 * h + 8:16 * h + 10, 16 * h] = z[:, None, None]
    return {**d, "x": np.ascontiguousarray(a[:, :, :4 * C]), "gh": np.ascontiguousarray(a[:, :, 4 * C:]), **lists_of(rng, (), (full,)), **still(rng)}
def setup_inputs_huge(rng):
    d = numbers_of(rng)
    a = 2.0 ** 29 * (0.6 + 0.4 * rng.random((N, 128, C + G, 4)))
    c = np.stack([rng.permutation(C + G) % 2 * 2.0 - 1.0 for r in range(N)])
    one = rng.permutation(N) < N // 2
    c[one] = 1
    a = (a * c[:, None, :, None]).astype(np.float32).reshape(N, 128, 4 * (C + G)).astype(BF)
    z = 2.0 ** 30 * (1 - 0.25 * rng.random((N, 128, 8, 4))) * signs(rng)[:, None, :, None]
    d["u"].reshape(N, 128, 128, 4)[:, :, ::16] = z.astype(np.float32).astype(BF)
    return {**d, "x": np.ascontiguousarray(a[:, :, :4 * C]), "gh": np.ascontiguousarray(a[:, :, 4 * C:]), **lists_of(rng, np.flatnonzero(~one)), **still(rng)}
def setup_inputs_shapes(rng):
    e = rng.permutation(N)
    kinds = np.stack([rng.permutation(8) for r in range(N)])
    kinds[e[0]] = 2
    kinds[e[1]] = 3
    nx = np.stack([linked(rng, kinds[r, g]) for r in range(N) for g in range(8)]).reshape(N, 8, C + G)
    j = np.arange(C)
    pr = np.zeros((N, 8, R, C), int)
    for r in range(N):
        o = rng.permutation(8)
        for g in range(8):
            for t in range(R): pr[r, g, t] = (j, j ^ 1, C - 1 - j, matching(rng, C // 2))[(o[g] + t) % 4]
    return {**numbers_of(rng), **stored(nx, pr), **weights(rng, f(rng, 128, 2048))}
def setup_inputs_spread(rng):
    d = setup_inputs(rng)
    d["x"] = big(wide(rng, N, 128, 4 * C, cols=6), 1)
    d["gh"] = big(wide(rng, N, 128, 4 * G, cols=6), 1)
    return d
def check_inputs(d):
    b = []
    for k in ("x", "gh", "u", "v"):
        a = np.abs(d[k].astype(np.float32))
        if not (np.isfinite(a).all() and ((a == 0) | (a >= 2.0 ** -30) & (a <= 2.0 ** 30)).all()): b.append("a value of " + k)
    for r in range(N):
        if (np.sort(gentries(d["nx"][r]), axis=1) != np.arange(C + G)).any(): b.append("nx of rank %d is no permutation in some group" % r)
        p = gentries(d["pr"][r]).reshape(8, R, C)
        if (p < 0).any() or (p >= C).any(): b.append("pr of rank %d out of range" % r)
        elif (np.take_along_axis(p, p, axis=2) != np.arange(C)).any(): b.append("pr of rank %d: a partner's partner is another column" % r)
    if (d["wc"] != d["wc"][:1]).any(): b.append("wc differs between ranks")
    s = [mx_ref.live(p) for p in d["ws"]]
    if any((p != s[0]).any() for p in s): b.append("ws differs between ranks")
    return b
def read(X, n):
    p = np.argsort(n, axis=1)
    return (gcols(X, n[:, :C]).astype(np.float32) + gcols(X, p[:, :C]).astype(np.float32)).astype(BF)
def reference(x, gh, u, v, nx, pr, wc, ws):
    w = pk(wc[0], ws[0])
    layer = [pick(w, np.arange(128 * b, 128 * b + 128)) for b in range(4)]
    qu = [mx_ref.quantize(u[r]) for r in range(N)]
    now = [np.concatenate([x[r], gh[r]], axis=1) for r in range(N)]
    link = [gentries(nx[r]) for r in range(N)]
    pair = [gentries(pr[r]).reshape(8, R, C) for r in range(N)]
    j = np.arange(C)
    for t in range(R):
        made = []
        for r in range(N):
            q = mx_ref.quantize(read(now[r], link[r]))
            s = mx_ref.matmul(qu[r], q)[::16] + np.float32(0.0)
            a, n = pair[r][:, t], link[r][:, :C]
            o = np.take_along_axis(s, a, axis=1)
            swap = (j < a) & (s < o) | (j > a) & (o < s)
            link[r] = np.concatenate([np.where(swap, np.take_along_axis(n, a, axis=1), n), link[r][:, C:]], axis=1)
            h = tile([np.maximum(mx_ref.matmul(layer[b], q), np.float32(0.0)) * np.float32(0.015625) for b in range(4)])
            made.append(decode(mx_ref.quantize(h)).astype(BF))
        for r in range(N):
            now[r] = np.concatenate([made[r], cut(made[r ^ (1 << t % L)], 0, 4 * G)], axis=1)
    y, nl = np.zeros((N, 128, C), np.float32), np.zeros((N, 8, C + G), np.float32)
    oc, osc = np.zeros((N, 128, 4 * C), np.uint8), np.zeros((N, 16, C), np.uint8)
    for r in range(N):
        q = mx_ref.quantize(read(now[r], link[r]))
        y[r] = mx_ref.matmul(mx_ref.quantize(v[r]), q)
        nl[r] = link[r]
        oc[r], osc[r] = emit(q)
    return {"y": y, "nl": nl, "oc": oc, "osc": osc}

@@ -1,0 +1,467 @@
+from concourse.bass import DstId, RemoteDMATransfer
+from concourse.mybir import dt, AluOpType, ActivationFunctionType
+
+C, G, R, WIN = 384, 192, 3, 576
+H = G
+STEP, KILL = 1000, 65536
+F8, BF, F32, I32, U16, U8 = "float8_e4m3fn_x4", "bfloat16", "float32", "int32", "uint16", "uint8"
+
+SCRATCH = {
+    "nxi": ("sbuf", [128, 36], I32), "pri": ("sbuf", [128, 72], I32), "xw": ("sbuf", [128, 4 * WIN], BF),
+    "ut": ("sbuf", [128, 512], BF), "vt": ("sbuf", [128, 512], BF), "wq": ("sbuf", [128, 512], F8), "wsc": ("sbuf", [128, 512], U8),
+    "J": ("sbuf", [128, WIN], F32), "J2": ("sbuf", [128, C], F32), "pi": ("sbuf", [128, 1], I32), "qi": ("sbuf", [128, 1], I32), "qf": ("sbuf", [128, 1], F32),
+    "kq": ("sbuf", [128, 1], F32), "t4": ("sbuf", [128, 4], F32), "kq4": ("sbuf", [128, 4], F32), "jm": ("sbuf", [128, C], F32),
+    "cm": ("sbuf", [128, C], F32), "cc": ("sbuf", [128, C], F32), "jo": ("sbuf", [128, 72], F32), "joq": ("sbuf", [128, 72], F32),
+    "uo": ("sbuf", [128, 8], I32), "uof": ("sbuf", [128, 8], U16),
+    "ones": ("sbuf", [128, 528], BF), "ee": ("sbuf", [128, 528], BF),
+    "eq": ("sbuf", [128, 512], F8), "es": ("sbuf", [128, 512], U8),
+    "uq": ("sbuf", [128, 128], F8), "us": ("sbuf", [128, 128], U8), "uq16": ("sbuf", [128, 128], F8), "us16": ("sbuf", [128, 128], U8),
+    "vq": ("sbuf", [128, 128], F8), "vs": ("sbuf", [128, 128], U8),
+    "nxo": ("sbuf", [128, 36], U16), "nx4": ("sbuf", [128, 96], U16), "pv4": ("sbuf", [128, 96], U16),
+    "pvo": ("sbuf", [128, 96], U16), "nxl": ("sbuf", [128, 96], U16), "pro": ("sbuf", [128, 72], U16),
+    "prf": ("sbuf", [128, 72], F32), "dpr": ("sbuf", [128, 72], F32), "kd": ("sbuf", [128, 72], F32), "base": ("sbuf", [128, 72], F32),
+    "nxr": ("sbuf", [128, WIN + 3 * C], F32), "pvr": ("sbuf", [128, WIN], F32), "sg": ("sbuf", [128, WIN], F32),
+    "df": ("sbuf", [128, 3 * C], F32), "D": ("sbuf", [128, 3 * C], F32),
+    "T1": ("sbuf", [128, C], F32), "NT1": ("sbuf", [128, C], F32), "sw": ("sbuf", [128, C], F32),
+    "scs": ("sbuf", [128, C], F32), "scn": ("sbuf", [128, C], F32), "scp": ("sbuf", [128, C], F32), "pvx": ("sbuf", [128, C], F32),
+    "ta": ("sbuf", [128, 72], F32), "tb": ("sbuf", [128, 72], F32), "so": ("sbuf", [128, 72], U16),
+    "y_sb": ("sbuf", [128, C], F32),
+}
+for _t in range(R + 1):
+    SCRATCH["P%d" % _t] = ("sbuf", [128, 4 * C], BF)
+    SCRATCH["z%d" % _t] = ("sbuf", [128, 4 * C], BF)
+    SCRATCH["zq%d" % _t] = ("sbuf", [128, C], F8)
+    SCRATCH["zs%d" % _t] = ("sbuf", [128, C], U8)
+    if _t < R:
+        SCRATCH["win%d" % (_t + 1)] = ("sbuf", [128, 4 * WIN], BF)
+        SCRATCH["h%d" % _t] = ("sbuf", [128, 4 * C], BF)
+        SCRATCH["hq%d" % _t] = ("sbuf", [128, C], F8)
+        SCRATCH["hs%d" % _t] = ("sbuf", [128, C], U8)
+        SCRATCH["rc%d" % _t] = ("sbuf", [128, G // 2], F8)
+        SCRATCH["rs%d" % _t] = ("sbuf", [128, G], U8)
+        SCRATCH["gq%d" % _t] = ("sbuf", [128, G], F8)
+        SCRATCH["gs%d" % _t] = ("sbuf", [128, G], U8)
+for _b in range(8):
+    SCRATCH["pb%d" % _b] = ("psum", [128, 512], F32)
+
+SEMAPHORES = (["c%d" % i for i in range(100)] + ["d%d" % i for i in range(30)]
+              + ["rarr%d" % t for t in range(R)] + ["garr%d" % t for t in range(R)] + ["sent"])
+
+
+def mask_of(engines):
+    m = 0
+    for e in engines:
+        m |= 1 << e
+    return m
+
+
+def relays_of(core, dest, topo):
+    c = [k for k in topo.cores_of(core) if k != core and topo.may_write(k, dest)]
+    near = [k for k in c if topo.die(k) == topo.die(core)]
+    far = [k for k in c if topo.die(k) != topo.die(core)]
+    return [near[0], far[0], near[1]]
+
+
+def hop_engines(core, relays, topo):
+    e0, e1, e2 = (topo.engines(core, k) for k in relays)
+    h = len(e0) // 2
+    return [e0[:h], e1[h:], e2]
+
+
+def relay_program(g, core, T, topo):
+    mine = [c for c in T.cores if c in topo.cores_of(core)]
+    if not mine:
+        return
+    src = mine[0]
+    r = T.rank_of(src)
+    total = 0
+    for t in range(R):
+        dest = T.cores[r ^ (1 << t)]
+        rel = relays_of(src, dest, topo)
+        if core not in rel:
+            continue
+        k = rel.index(core)
+        rid, pid = topo.addr(dest, core)
+        if k < 2:
+            a, b = k * (G // 2), (k + 1) * (G // 2)
+            out, inn = T["gq%d" % t][:, a:b].bitcast(dt.uint8), T["rc%d" % t][:, :].bitcast(dt.uint8)
+        else:
+            out, inn = T["gs%d" % t][:, :], T["rs%d" % t][:, :]
+        g.wait_ge(T.sem["rarr%d" % t], len(hop_engines(src, rel, topo)[k]))
+        g.remote_dma(out, inn, T.sem["garr%d" % t], T.sem["sent"], pid, rid, topo.mask(core, dest))
+        total += len(topo.engines(core, dest))
+    if total:
+        g.wait_ge(T.sem["sent"], total)
+
+
+def emit(g, T, ops):
+    queues = {"g": g, "v": g.vector, "s": g.scalar, "p": g.tensor, "y": g.sync}
+    hist, know, at, need = {}, {q: set() for q in queues}, [], []
+    used = set()
+    for i, o in enumerate(ops):
+        deps = set()
+        for k, lo, hi in o["r"]:
+            for (a, b, j, wr) in hist.get(k, ()):
+                if wr and a < hi and lo < b:
+                    deps.add(j)
+        for k, lo, hi in o["w"]:
+            for (a, b, j, wr) in hist.get(k, ()):
+                if a < hi and lo < b:
+                    deps.add(j)
+        for k, lo, hi in o["w"]:
+            lst = hist.setdefault(k, [])
+            lst[:] = [e for e in lst if not (lo <= e[0] and e[1] <= hi)]
+            lst.append((lo, hi, i, True))
+        for k, lo, hi in o["r"]:
+            hist.setdefault(k, []).append((lo, hi, i, False))
+        deps.discard(i)
+        if o["q"] is None:
+            at.append(set())
+            need.append([])
+            continue
+        kq, w = know[o["q"]], []
+        for j in sorted(deps, reverse=True):
+            if j in kq:
+                continue
+            w.append(j)
+            used.add(j)
+            kq.add(j)
+            kq |= at[j]
+        need.append(w)
+        at.append(set(kq))
+    last, count, sem = {}, {}, {}
+    for i, o in enumerate(ops):
+        if i not in used:
+            continue
+        if o["q"] is None:
+            sem[i] = (o["sem"], o["val"])
+            continue
+        kind, n = ("d", 16) if o.get("dma") else ("c", 1)
+        k = 0
+        while (kind, k) in last and last[(kind, k)] not in at[i]:
+            k += 1
+        last[(kind, k)] = i
+        count[(kind, k)] = count.get((kind, k), 0) + n
+        sem[i] = ("%s%d" % (kind, k), count[(kind, k)])
+    for i, o in enumerate(ops):
+        if o["q"] is None:
+            continue
+        e = queues[o["q"]]
+        for j in need[i]:
+            e.wait_ge(T.sem[sem[j][0]], sem[j][1])
+        if o["f"] is None:
+            continue
+        ins = o["f"](e)
+        if i in sem:
+            ins.then_inc(T.sem[sem[i][0]], 16 if o.get("dma") else 1)
+
+
+def rank_program(g, core, T, topo):
+    rank = T.rank_of(core)
+    if rank is None:
+        return relay_program(g, core, T, topo)
+    ops = []
+    ADD, SUB, MUL, MAX = AluOpType.add, AluOpType.subtract, AluOpType.mult, AluOpType.max
+    GT, LT, AND = AluOpType.is_gt, AluOpType.is_lt, AluOpType.bitwise_and
+    ACT = ActivationFunctionType
+
+    def op(q, f, r=(), w=(), **kw):
+        ops.append(dict(q=q, f=f, r=list(r), w=list(w), **kw))
+
+    def full(*names):
+        return [(n, 0, 1 << 20) for n in names]
+
+    def move(q, out, src, r, w):
+        op(q, lambda e: e.dma_start(out, src), r, w, dma=True)
+
+    def copy(q, out, in_, r, w):
+        if q == "s":
+            op("s", lambda e: e.activation(out, in_, ACT.Copy), r, w)
+        else:
+            op("v", lambda e: e.tensor_copy(out, in_), r, w)
+
+    def tt(out, a, b, o, r, w):
+        op("v", lambda e: e.tensor_tensor(out, a, b, o), r, w)
+
+    def ts(out, a, s1, s2, o1, o2, r, w):
+        if o2 is None:
+            op("v", lambda e: e.tensor_scalar(out, a, s1, None, o1), r, w)
+        else:
+            op("v", lambda e: e.tensor_scalar(out, a, s1, s2, o1, o2), r, w)
+
+    def iota(out, pat, base, cm, w, small=True):
+        if small:
+            op("g", lambda e: e.iota(out, pat, base, cm, allow_small_or_imprecise_dtypes=True), (), w)
+        else:
+            op("g", lambda e: e.iota(out, pat, base, cm), (), w)
+
+    def quant(qn, sn, a, b, src, lo, hi, r):
+        op("v", lambda e: e.quantize_mx(T[qn][:, a:b], T[sn][:, a:b], T[src][:, lo:hi]), r, [(qn, a, b)])
+
+    bank = [0]
+
+    def mm(wn, wsn, wa, xn, xsn, a, b):
+        k = "pb%d" % bank[0]
+        bank[0] = (bank[0] + 1) % 8
+        out = T[k][:, 0:b - a]
+        op("p", lambda e: e.matmul_mx(out, T[wn][:, wa:wa + 128], T[wsn][:, wa:wa + 128], T[xn][:, a:b], T[xsn][:, a:b], True, True),
+           [(wn, wa, wa + 128), (wsn + ".load", 0, 1), (xn, a, b)], full(k))
+        return out, k
+
+    def offs(name, i, lo, n):
+        return T[name][:, 24 * i + lo // 16:24 * i + (lo + n) // 16]
+
+    def window(t, b):
+        if t == 0:
+            return T.xw[:], ("xw", 0, 4 * WIN)
+        return T["win%d" % t][:, WIN * b:WIN * b + WIN], ("win%d" % t, WIN * b, WIN * b + WIN)
+
+    def stage(t, b, lo, n):
+        ls, i = ("nx4", b) if t == 0 else ("pvo", t)
+        w, key = window(t, b)
+        out, off = T["P%d" % t][:, C * b + lo:C * b + lo + n], offs(ls, i, lo, n)
+        op("s", lambda e: e.activation(out, w.indirect(off), ACT.Copy), [(ls, i, i + 1), key], [("P%d" % t, C * b + lo, C * b + lo + n)])
+
+    def read(t, b, lo, n):
+        ls, i = ("pv4", b) if t == 0 else ("nxl", t)
+        w, key = window(t, b)
+        tt(T["z%d" % t][:, 4 * lo + b:4 * (lo + n):4], w.indirect(offs(ls, i, lo, n)), T["P%d" % t][:, C * b + lo:C * b + lo + n], ADD,
+           [(ls, i, i + 1), key, ("P%d" % t, C * b + lo, C * b + lo + n)], [("z%d.%d" % (t, b), lo, lo + n)])
+
+    def quant_z(t, lo, n):
+        quant("zq%d" % t, "zs%d" % t, lo, lo + n, "z%d" % t, 4 * lo, 4 * (lo + n), [("z%d.%d" % (t, b), lo, lo + n) for b in range(4)])
+
+    def layer(t, b, lo, n):
+        return mm("wq", "wsc", 128 * b, "zq%d" % t, "zs%d" % t, lo, lo + n)
+
+    def relu(q, t, b, lo, n, pk):
+        out = T["h%d" % t][:, 4 * lo + b:4 * (lo + n):4]
+        w = [("h%d.%d" % (t, b), lo, lo + n)]
+        if q == "s":
+            op("s", lambda e: e.activation(out, pk[0], ACT.Relu, scale=0.015625), full(pk[1]), w)
+        else:
+            ts(out, pk[0], 0.0, 0.015625, MAX, MUL, full(pk[1]), w)
+
+    def quant_h(t, lo, n):
+        quant("hq%d" % t, "hs%d" % t, lo, lo + n, "h%d" % t, 4 * lo, 4 * (lo + n), [("h%d.%d" % (t, b), lo, lo + n) for b in range(4)])
+
+    def unpack(b, xn, xsn, lo, n):
+        return mm("eq", "es", 128 * b, xn, xsn, lo, lo + n)
+
+    def put(q, t, b, lo, n, pk):
+        a = WIN * b + lo
+        copy(q, T["win%d" % t][:, a:a + n], pk[0], full(pk[1]), [("win%d" % t, a, a + n)])
+
+    def send(t):
+        dest = T.cores[rank ^ (1 << t)]
+        rel = relays_of(core, dest, topo)
+        en = hop_engines(core, rel, topo)
+        ids = [topo.addr(k, core) for k in rel]
+        hq, hs, rc, rs = T["hq%d" % t], T["hs%d" % t], T["rc%d" % t], T["rs%d" % t]
+        h = G // 2
+
+        def f(e):
+            e.remote_dma_fused([RemoteDMATransfer(dst_ids=[DstId(rid=ids[k][0], pnc=ids[k][1])], dma_engine_mask=mask_of(en[k]), remote_sem=T.sem["rarr%d" % t],
+                                                  src=hq[:, h * k:h * k + h].bitcast(dt.uint8), dst=rc[:, :].bitcast(dt.uint8)) for k in range(2)], local_sem=T.sem["sent"])
+            return e.remote_dma(rs[:, :], hs[:, 0:G], T.sem["rarr%d" % t], T.sem["sent"], ids[2][1], ids[2][0], mask_of(en[2]))
+        op("g", f, [("hq%d" % t, 0, G)], ())
+        return sum(len(x) for x in en)
+
+    def arrive(t):
+        far = T.cores[rank ^ (1 << t)]
+        op(None, None, (), full("gq%d" % t), sem="garr%d" % t, val=sum(len(topo.engines(k, core)) for k in relays_of(far, core, topo)))
+
+    def scan(dst, src, a, r):
+        op("v", lambda e: e.tensor_tensor_scan(T[dst][:], T.cc[:], T[src][:, a:a + C], 0.0, ADD, MAX), r + full("cc"), full(dst))
+
+    def signs(k):
+        o = C * k
+        tt(T.df[:, o:o + C], T.J[:, 0:C].indirect(T.pro[:, 24 * k:24 * k + 24]), T.J2[:], SUB, full("J", "J2", "pro"), [("df", k, k + 1)])
+        op("s", lambda e: e.activation(T.D[:, o:o + C], T.df[:, o:o + C], ACT.Sign), [("df", k, k + 1)], [("D", k, k + 1)])
+
+    def score(t, lo, n, pk):
+        o = C * t + lo
+        tt(T.T1[:, lo:lo + n], pk[0], T.D[:, o:o + n], MUL, full(pk[1]) + [("D", t, t + 1)], [("T1", lo, lo + n)])
+
+    def swaps(t):
+        tt(T.sw[:], T.T1[:].indirect(T.pro[:, 24 * t:24 * t + 24]), T.NT1[:], LT, full("T1", "NT1", "pro"), full("sw"))
+        scan("scs", "sw", 0, full("sw"))
+        a = slice(24 * t, 24 * t + 24)
+        tt(T.ta[:, a], T.scs[:, 15:C:16], T.dpr[:, a], MUL, full("scs", "dpr"), [("ta", t, t + 1)])
+        tt(T.tb[:, a], T.ta[:, a], T.base[:, a], ADD, [("ta", t, t + 1)] + full("base"), [("tb", t, t + 1)])
+        copy("v", T.so[:, a], T.tb[:, a], [("tb", t, t + 1)], [("so", t, t + 1)])
+
+    def nxrow(t):
+        return (0, C) if t == 0 else (WIN + C * (t - 1), WIN + C * t)
+
+    def swap_rows_s(t):
+        so = T.so[:, 24 * t:24 * t + 24]
+        op("s", lambda e: e.activation(T.sg[:, 0:C], T.J[:, 0:C].indirect(so), ACT.Copy), [("so", t, t + 1)] + full("J"), [("sg", 0, C)])
+
+    def swap_rows_pv(t):
+        op("s", lambda e: e.activation(T.pvx[:], T.sg[:].indirect(T.pvo[:, 24 * t:24 * t + 24]), ACT.Copy), [("pvo", t, t + 1), ("sg", 0, WIN)], full("pvx"))
+
+    def swap_rows_nx(t):
+        so = T.so[:, 24 * t:24 * t + 24]
+        a, b = nxrow(t)
+        c, d = nxrow(t + 1)
+        op("v", lambda e: e.tensor_copy(T.nxr[:, c:d], T.nxr[:, a:b].indirect(so)), [("so", t, t + 1), ("nxr", a, b)], [("nxr", c, d)])
+
+    def list_pv(t):
+        scan("scp", "pvx", 0, full("pvx"))
+        ts(T.pvo[:, 24 * t + 24:24 * t + 48], T.scp[:, 15:C:16], T.kq[:, 0:1], None, SUB, None, full("scp", "kq"), [("pvo", t + 1, t + 2)])
+
+    def list_nx(t):
+        c, d = nxrow(t + 1)
+        scan("scn", "nxr", c, [("nxr", c, d)])
+        ts(T.nxl[:, 24 * t + 24:24 * t + 48], T.scn[:, 15:C:16], T.kq[:, 0:1], None, SUB, None, full("scn", "kq"), [("nxl", t + 1, t + 2)])
+
+    move("y", T.nxi[:], T.nx[:], (), full("nxi"))
+    move("y", T.xw[:, 0:4 * C], T.x[:], (), [("xw", 0, 4 * C)])
+    move("y", T.xw[:, 4 * C:4 * WIN], T.gh[:], (), [("xw", 4 * C, 4 * WIN)])
+    move("y", T.pri[:], T.pr[:], (), full("pri"))
+    move("y", T.wq[:].bitcast(dt.uint8), T.wc[:], (), full("wq"))
+    move("y", T.wsc[:], T.ws[:], (), full("wsc.load"))
+    move("y", T.ut[:], T.u[:], (), full("ut"))
+    move("y", T.vt[:], T.v[:], (), full("vt"))
+
+    iota(T.pi[:], [[0, 1]], 0, 1, full("pi"), small=False)
+    iota(T.t4[:], [[1, 4]], 0, 0, full("t4"))
+    iota(T.jm[:], [[0, C // 16], [1, 16]], 0, 0, full("jm"))
+    iota(T.J[:], [[1, WIN]], 0, 0, full("J"))
+    iota(T.jo[:], [[0, R], [16, 24]], 0, 0, full("jo"))
+    iota(T.sg[:, C:WIN], [[1, G]], C, 0, [("sg", C, WIN)])
+    iota(T.uo[:], [[16, 8]], 0, 0, full("uo"), small=False)
+    op("v", lambda e: e.memset(T.ones[:], 1.0), (), full("ones"))
+    op("g", lambda e: e.affine_select(T.ee[:], T.ones[:], [[-1, 528]], AluOpType.is_equal, 0.0, 4, 4), full("ones"), full("ee"))
+    iota(T.J2[:], [[1, C]], 0, 0, full("J2"))
+    ts(T.qi[:], T.pi[:], 15, None, AND, None, full("pi"), full("qi"))
+    copy("v", T.qf[:], T.qi[:], full("qi"), full("qf"))
+    ts(T.kq[:], T.qf[:], -float(STEP), 15.0 * STEP, MUL, ADD, full("qf"), full("kq"))
+    ts(T.cm[:], T.jm[:], T.qf[:, 0:1], float(KILL + STEP), GT, MUL, full("jm", "qf"), full("cm"))
+    ts(T.cc[:], T.cm[:], -float(KILL), None, ADD, None, full("cm"), full("cc"))
+    ts(T.kq4[:], T.t4[:], -0.25, T.kq[:, 0:1], MUL, ADD, full("t4", "kq"), full("kq4"))
+
+    copy("v", T.nxo[:], T.nxi[:], full("nxi"), full("nxo"))
+    for b in range(4):
+        ts(T.nx4[:, 24 * b:24 * b + 24], T.nxi[:, 0:24], 4.0, float(b), MUL, ADD, full("nxi"), [("nx4", b, b + 1)])
+    op("v", lambda e: e.tensor_copy(T.pvr[:].indirect(T.nxo[:]), T.J[:]), full("J", "nxo"), full("pvr"))
+    op("s", lambda e: e.activation(T.nxr[:, 0:WIN], T.J[:].indirect(T.nxo[:]), ACT.Copy), full("J", "nxo"), [("nxr", 0, WIN)])
+    for b in range(4):
+        stage(0, b, 0, H)
+    scan("scp", "pvr", 0, full("pvr"))
+    for b in range(4):
+        ts(T.pv4[:, 24 * b:24 * b + 24], T.scp[:, 15:C:16], T.kq4[:, b:b + 1], 4.0, SUB, MUL, full("scp", "kq4"), [("pv4", b, b + 1)])
+
+    sent = 0
+    for t in range(R):
+        lo2, n2 = H, C - H
+        if t:
+            arrive(t - 1)
+            gk = [unpack(b, "gq%d" % (t - 1), "gs%d" % (t - 1), 0, G) for b in range(4)]
+            for b in range(4):
+                put("v", t, b, C, G, gk[b])
+            for b in range(4):
+                stage(t, b, 0, H)
+        for b in range(4):
+            read(t, b, 0, H)
+        for b in range(3):
+            stage(t, b, lo2, n2)
+        quant_z(t, 0, H)
+        k1 = [layer(t, b, 0, H) for b in range(4)]
+        if t == 0:
+            copy("v", T.pro[:], T.pri[:], full("pri"), full("pro"))
+            copy("v", T.prf[:], T.pri[:], full("pri"), full("prf"))
+            ts(T.joq[:], T.jo[:], T.qf[:, 0:1], None, ADD, None, full("jo", "qf"), full("joq"))
+            tt(T.dpr[:], T.prf[:], T.joq[:], SUB, full("prf", "joq"), full("dpr"))
+            ts(T.kd[:], T.dpr[:], T.kq[:, 0:1], None, MUL, None, full("dpr", "kq"), full("kd"))
+        relu("s", t, 0, 0, H, k1[0])
+        if t:
+            read(t, 0, lo2, n2)
+        relu("v", t, 1, 0, H, k1[1])
+        relu("s", t, 2, 0, H, k1[2])
+        relu("v", t, 3, 0, H, k1[3])
+        quant_h(t, 0, H)
+        sent += send(t)
+        if t == 0:
+            ts(T.pvo[:, 0:24], T.scp[:, 15:C:16], T.kq[:, 0:1], None, SUB, None, full("scp", "kq"), [("pvo", 0, 1)])
+            tt(T.base[:], T.joq[:], T.kd[:], SUB, full("joq", "kd"), full("base"))
+            read(0, 0, lo2, n2)
+        else:
+            ks = mm("uq16", "us16", 0, "zq%d" % t, "zs%d" % t, 0, H)
+        stage(t, 3, lo2, n2)
+        for b in range(1, 4):
+            read(t, b, lo2, n2)
+        quant_z(t, lo2, n2)
+        if t == 0:
+            quant("uq", "us", 0, 128, "ut", 0, 512, full("ut"))
+            copy("v", T.uof[:], T.uo[:], full("uo"), full("uof"))
+            op("v", lambda e: e.tensor_copy(T.uq16[:, 0:128].bitcast(dt.uint32), T.uq[:, 0:128].bitcast(dt.uint32).indirect(T.uof[:, 0:8])), full("uq", "uof"), full("uq16.q"))
+            op("v", lambda e: e.tensor_copy(T.us16[:, 0:128], T.us[:, 0:128].indirect(T.uof[:, 0:8])), full("uq", "uof", "uq16.q"), full("uq16"))
+            ks = mm("uq16", "us16", 0, "zq0", "zs0", 0, H)
+            for b in range(4):
+                quant("eq", "es", 128 * b, 128 * b + 128, "ee", 4 - b, 516 - b, full("ee"))
+        kt = mm("uq16", "us16", 0, "zq%d" % t, "zs%d" % t, lo2, C)
+        k2 = [layer(t, b, lo2, n2) for b in range(4)]
+        if t == 0:
+            signs(0)
+        score(t, 0, H, ks)
+        score(t, lo2, n2, kt)
+        op("s", lambda e: e.activation(T.NT1[:], T.T1[:], ACT.Copy, scale=-1.0), full("T1"), full("NT1"))
+        if t + 1 < R:
+            signs(t + 1)
+        ka = [unpack(b, "hq%d" % t, "hs%d" % t, 0, H) for b in range(4)]
+        for b in range(4):
+            relu("s", t, b, lo2, n2, k2[b])
+        swaps(t)
+        quant_h(t, lo2, n2)
+        put("s", t + 1, 0, 0, H, ka[0])
+        swap_rows_s(t)
+        swap_rows_pv(t)
+        put("s", t + 1, 1, 0, H, ka[1])
+        swap_rows_nx(t)
+        put("s", t + 1, 2, 0, H, ka[2])
+        kb = [unpack(b, "hq%d" % t, "hs%d" % t, lo2, n2) for b in range(4)]
+        put("v", t + 1, 3, 0, H, ka[3])
+        list_nx(t)
+        put("s", t + 1, 0, lo2, n2, kb[0])
+        put("s", t + 1, 1, lo2, n2, kb[1])
+        list_pv(t)
+        put("s", t + 1, 2, lo2, n2, kb[2])
+        put("s", t + 1, 3, lo2, n2, kb[3])
+        if t == 0:
+            quant("vq", "vs", 0, 128, "vt", 0, 512, full("vt"))
+            move("y", T.nl[:, C:WIN], T.nxr[0:128:16, C:WIN], [("nxr", C, WIN)], [("nl", C, WIN)])
+        if t == R - 1:
+            c, d = nxrow(R)
+            move("y", T.nl[:, 0:C], T.nxr[0:128:16, c:d], [("nxr", c, d)], [("nl", 0, C)])
+
+    t, cut = R, 256
+    zq, zs = T["zq%d" % R], T["zs%d" % R]
+    arrive(R - 1)
+    gk = [unpack(b, "gq%d" % (R - 1), "gs%d" % (R - 1), 0, G) for b in range(4)]
+    for b in range(4):
+        put("v", t, b, C, G, gk[b])
+    for b in range(4):
+        stage(t, b, 0, cut)
+    for b in range(4):
+        read(t, b, 0, cut)
+    quant_z(t, 0, cut)
+    k1 = mm("vq", "vs", 0, "zq%d" % R, "zs%d" % R, 0, cut)
+    move("y", T.oc[:, 0:4 * cut], zq[:, 0:cut].bitcast(dt.uint8), [("zq%d" % R, 0, cut)], [("oc", 0, cut)])
+    for b in range(4):
+        stage(t, b, cut, C - cut)
+    for b in range(4):
+        read(t, b, cut, C - cut)
+    copy("s", T.y_sb[:, 0:cut], k1[0], full(k1[1]), [("y_sb", 0, cut)])
+    move("y", T.y[:, 0:cut], T.y_sb[:, 0:cut], [("y_sb", 0, cut)], [("y", 0, cut)])
+    quant_z(t, cut, C - cut)
+    k2 = mm("vq", "vs", 0, "zq%d" % R, "zs%d" % R, cut, C)
+    move("y", T.oc[:, 4 * cut:4 * C], zq[:, cut:C].bitcast(dt.uint8), [("zq%d" % R, cut, C)], [("oc", cut, C)])
+    for k in range(4):
+        move("s", T.osc[4 * k:4 * k + 4, :], zs[32 * k:32 * k + 4, :], [("zq%d" % R, 0, C)], [("osc", k, k + 1)])
+    copy("v", T.y_sb[:, cut:C], k2[0], full(k2[1]), [("y_sb", cut, C)])
+    move("y", T.y[:, cut:C], T.y_sb[:, cut:C], [("y_sb", cut, C)], [("y", cut, C)])
+    op("y", None, [("oc", 0, C), ("y", 0, C), ("osc", 0, 4), ("nl", 0, WIN)], ())
+    emit(g, T, ops)
+    g.wait_ge(T.sem.sent, sent)

@@ -5,42 +5,26 @@ C, G, R, WIN = 384, 192, 3, 576
 H = G
 STEP, KILL = 1000, 65536
 F8, BF, F32, I32, U16, U8 = "float8_e4m3fn_x4", "bfloat16", "float32", "int32", "uint16", "uint8"
+CY, GATHER, SCATTER, WAKE, HOPS, FIRST, LOOK, URGENT, EASY = 0.0011, 1.5, 3.6, 0.1, 5.0, 3.0, 0.25, 0.2, 1.0
+PUT_Q, STAGE_Q, RELU_Q = "vsvv", "ssss", "svsv"
 
-SCRATCH = {
-    "nxi": ("sbuf", [128, 36], I32), "pri": ("sbuf", [128, 72], I32), "xw": ("sbuf", [128, 4 * WIN], BF),
-    "ut": ("sbuf", [128, 512], BF), "vt": ("sbuf", [128, 512], BF), "wq": ("sbuf", [128, 512], F8), "wsc": ("sbuf", [128, 512], U8),
-    "J": ("sbuf", [128, WIN], F32), "J2": ("sbuf", [128, C], F32), "pi": ("sbuf", [128, 1], I32), "qi": ("sbuf", [128, 1], I32), "qf": ("sbuf", [128, 1], F32),
-    "kq": ("sbuf", [128, 1], F32), "t4": ("sbuf", [128, 4], F32), "kq4": ("sbuf", [128, 4], F32), "jm": ("sbuf", [128, C], F32),
-    "cm": ("sbuf", [128, C], F32), "cc": ("sbuf", [128, C], F32), "jo": ("sbuf", [128, 72], F32), "joq": ("sbuf", [128, 72], F32),
-    "uo": ("sbuf", [128, 8], I32), "uof": ("sbuf", [128, 8], U16),
-    "ones": ("sbuf", [128, 528], BF), "ee": ("sbuf", [128, 528], BF),
-    "eq": ("sbuf", [128, 512], F8), "es": ("sbuf", [128, 512], U8),
-    "uq": ("sbuf", [128, 128], F8), "us": ("sbuf", [128, 128], U8), "uq16": ("sbuf", [128, 128], F8), "us16": ("sbuf", [128, 128], U8),
-    "vq": ("sbuf", [128, 128], F8), "vs": ("sbuf", [128, 128], U8),
-    "nxo": ("sbuf", [128, 36], U16), "nx4": ("sbuf", [128, 96], U16), "pv4": ("sbuf", [128, 96], U16),
-    "pvo": ("sbuf", [128, 96], U16), "nxl": ("sbuf", [128, 96], U16), "pro": ("sbuf", [128, 72], U16),
-    "prf": ("sbuf", [128, 72], F32), "dpr": ("sbuf", [128, 72], F32), "kd": ("sbuf", [128, 72], F32), "base": ("sbuf", [128, 72], F32),
-    "nxr": ("sbuf", [128, WIN + 3 * C], F32), "pvr": ("sbuf", [128, WIN], F32), "sg": ("sbuf", [128, WIN], F32),
-    "df": ("sbuf", [128, 3 * C], F32), "D": ("sbuf", [128, 3 * C], F32),
-    "T1": ("sbuf", [128, C], F32), "NT1": ("sbuf", [128, C], F32), "sw": ("sbuf", [128, C], F32),
-    "scs": ("sbuf", [128, C], F32), "scn": ("sbuf", [128, C], F32), "scp": ("sbuf", [128, C], F32), "pvx": ("sbuf", [128, C], F32),
-    "ta": ("sbuf", [128, 72], F32), "tb": ("sbuf", [128, 72], F32), "so": ("sbuf", [128, 72], U16),
-    "y_sb": ("sbuf", [128, C], F32),
-}
+SCRATCH = {n: ("sbuf", [128, w], d) for n, w, d in (
+    ("nxi", 36, I32), ("pri", 72, I32), ("xw", 4 * WIN, BF), ("ut", 512, BF), ("vt", 512, BF), ("wq", 512, F8), ("wsc", 512, U8),
+    ("J", WIN, F32), ("J2", C, F32), ("pi", 1, I32), ("qi", 1, I32), ("qf", 1, F32), ("kq", 1, F32), ("kk", 1, F32), ("t4", 4, F32), ("kq4", 4, F32),
+    ("jm", C, F32), ("cm", C, F32), ("cc", C, F32), ("ccb", C, BF), ("jo", 72, F32), ("joq", 72, F32), ("uo", 8, I32), ("uof", 8, U16),
+    ("ones", 528, BF), ("ee", 528, BF), ("eq", 512, F8), ("es", 512, U8),
+    ("uq", 128, F8), ("us", 128, U8), ("uq16", 128, F8), ("us16", 128, U8), ("vq", 128, F8), ("vs", 128, U8),
+    ("nxo", 36, U16), ("nx4", 96, U16), ("pv4", 96, U16), ("pvo", 96, U16), ("nxl", 96, U16), ("pro", 72, U16), ("so", 72, U16),
+    ("prf", 72, F32), ("dpr", 72, F32), ("kd", 72, F32), ("base", 72, F32), ("ta", 72, F32), ("tb", 72, F32),
+    ("dn", 72, F32), ("dk", 72, F32), ("db", 72, F32), ("pa", 72, F32), ("pf", 96, F32),
+    ("nxr", WIN + 3 * C, F32), ("pvr", WIN, F32), ("df", 3 * WIN, F32), ("D", 3 * C, F32), ("T1", C, F32), ("NT1", C, F32),
+    ("sw", WIN, BF), ("swp", C, BF), ("scq", C, BF), ("scs", C, BF), ("scn", C, F32), ("scp", C, F32), ("dnr", C, F32), ("scd", C, F32), ("y_sb", C, F32))}
 for _t in range(R + 1):
-    SCRATCH["P%d" % _t] = ("sbuf", [128, 4 * C], BF)
-    SCRATCH["z%d" % _t] = ("sbuf", [128, 4 * C], BF)
-    SCRATCH["zq%d" % _t] = ("sbuf", [128, C], F8)
-    SCRATCH["zs%d" % _t] = ("sbuf", [128, C], U8)
+    SCRATCH.update({"%s%d" % (n, _t): ("sbuf", [128, w], d) for n, w, d in (("P", 4 * C, BF), ("z", 4 * C, BF), ("zq", C, F8), ("zs", C, U8))})
     if _t < R:
         SCRATCH["win%d" % (_t + 1)] = ("sbuf", [128, 4 * WIN], BF)
-        SCRATCH["h%d" % _t] = ("sbuf", [128, 4 * C], BF)
-        SCRATCH["hq%d" % _t] = ("sbuf", [128, C], F8)
-        SCRATCH["hs%d" % _t] = ("sbuf", [128, C], U8)
-        SCRATCH["rc%d" % _t] = ("sbuf", [128, G // 2], F8)
-        SCRATCH["rs%d" % _t] = ("sbuf", [128, G], U8)
-        SCRATCH["gq%d" % _t] = ("sbuf", [128, G], F8)
-        SCRATCH["gs%d" % _t] = ("sbuf", [128, G], U8)
+        SCRATCH.update({"%s%d" % (n, _t): ("sbuf", [128, w], d) for n, w, d in (
+            ("h", 4 * C, BF), ("hq", C, F8), ("hs", C, U8), ("rc", G // 2, F8), ("rs", G, U8), ("gq", G, F8), ("gs", G, U8))})
 for _b in range(8):
     SCRATCH["pb%d" % _b] = ("psum", [128, 512], F32)
 
@@ -94,20 +78,14 @@ def relay_program(g, core, T, topo):
         g.wait_ge(T.sem["sent"], total)
 
 
-def emit(g, T, ops):
-    queues = {"g": g, "v": g.vector, "s": g.scalar, "p": g.tensor, "y": g.sync}
-    hist, know, at, need = {}, {q: set() for q in queues}, [], []
-    used = set()
+def dependencies(ops):
+    hist, out = {}, []
     for i, o in enumerate(ops):
-        deps = set()
+        deps = set(o.get("after", ()))
         for k, lo, hi in o["r"]:
-            for (a, b, j, wr) in hist.get(k, ()):
-                if wr and a < hi and lo < b:
-                    deps.add(j)
+            deps |= {j for (a, b, j, wr) in hist.get(k, ()) if wr and a < hi and lo < b}
         for k, lo, hi in o["w"]:
-            for (a, b, j, wr) in hist.get(k, ()):
-                if a < hi and lo < b:
-                    deps.add(j)
+            deps |= {j for (a, b, j, wr) in hist.get(k, ()) if a < hi and lo < b}
         for k, lo, hi in o["w"]:
             lst = hist.setdefault(k, [])
             lst[:] = [e for e in lst if not (lo <= e[0] and e[1] <= hi)]
@@ -115,20 +93,91 @@ def emit(g, T, ops):
         for k, lo, hi in o["r"]:
             hist.setdefault(k, []).append((lo, hi, i, False))
         deps.discard(i)
+        out.append(deps)
+    return out
+
+
+def schedule(ops):
+    deps = dependencies(ops)
+    n = len(ops)
+    tail, readers = [0.0] * n, {}
+    for i in range(n - 1, -1, -1):
+        o = ops[i]
+        tail[i] += o["c"] + o.get("lat", 0.0)
+        for j in deps[i]:
+            tail[j] = max(tail[j], tail[i] + WAKE)
+        for k, lo, hi in o["r"]:
+            if k[0] == "@":
+                readers.setdefault(k, []).append(i)
+    prio = [o.get("prio", tail[i]) for i, o in enumerate(ops)]
+    free, end, start = {q: 0.0 for q in "gvspy"}, {}, {}
+    banks, todo = [None] * 8, list(range(n))
+
+    def bank_free(k):
+        return 0.0 if k is None else max(end[j] + WAKE for j in readers[k]) if all(j in end for j in readers[k]) else None
+    while todo:
+        cand, ready, arrived = {}, {}, None
+        for i in todo:
+            if any(j not in end for j in deps[i]):
+                continue
+            o = ops[i]
+            ready[i] = max([end[j] + WAKE for j in deps[i]] + [0.0])
+            if o["q"] is None:
+                start[i], end[i], arrived = ready[i], ready[i] + o.get("lat", 0.0), i
+                break
+            if "m" in o:
+                b = [x for x in map(bank_free, banks) if x is not None]
+                if not b:
+                    continue
+                ready[i] = max(ready[i], min(b))
+            for q in o["q"]:
+                cand.setdefault(q, []).append((max(free[q], ready[i]), i))
+        if arrived is not None:
+            todo.remove(arrived)
+            continue
+        own = max([prio[i] for s, i in cand.get("v", ()) if ops[i]["q"] == "v"] + [0.0])
+        cand["v"] = [(s, i) for s, i in cand.get("v", ()) if ops[i]["q"] == "v" or max(free["s"], ready[i]) > s + (URGENT if prio[i] > own else EASY)]
+        pick = None
+        for q, l in cand.items():
+            if l:
+                t0 = min(l)[0]
+                p, s, i = max((prio[i], -s, -i) for s, i in l if s <= t0 + LOOK)
+                if pick is None or (s, -p) > pick[:2]:
+                    pick = (s, -p, -i, q)
+        s, i, q = -pick[0], pick[2], pick[3]
+        o = ops[i]
+        if "m" in o:
+            x = min((bank_free(k), x) for x, k in enumerate(banks) if bank_free(k) is not None)[1]
+            banks[x] = o["w"][0][0]
+            o["m"]["k"] = "pb%d" % x
+        o["q"], start[i], free[q] = q, s, s + o["c"]
+        end[i] = free[q] + o.get("lat", 0.0)
+        todo.remove(i)
+    names = {o["w"][0][0]: o["m"]["k"] for o in ops if "m" in o}
+    for o in ops:
+        o["after"] = ()
+        for a in "rw":
+            o[a] = [(names.get(k, k), lo, hi) for k, lo, hi in o[a]]
+    return [ops[i] for i in sorted(range(n), key=lambda i: (start[i], i))]
+
+
+def emit(g, T, ops):
+    queues = {"g": g, "v": g.vector, "s": g.scalar, "p": g.tensor, "y": g.sync}
+    know, at, need, used = {q: set() for q in queues}, [], [], set()
+    for i, (o, deps) in enumerate(zip(ops, dependencies(ops))):
+        w = []
         if o["q"] is None:
             at.append(set())
-            need.append([])
-            continue
-        kq, w = know[o["q"]], []
-        for j in sorted(deps, reverse=True):
-            if j in kq:
-                continue
-            w.append(j)
-            used.add(j)
-            kq.add(j)
-            kq |= at[j]
+        else:
+            kq = know[o["q"]]
+            for j in sorted(deps, reverse=True):
+                if j not in kq:
+                    w.append(j)
+                    used.add(j)
+                    kq.add(j)
+                    kq |= at[j]
+            at.append(set(kq))
         need.append(w)
-        at.append(set(kq))
     last, count, sem = {}, {}, {}
     for i, o in enumerate(ops):
         if i not in used:
@@ -151,7 +200,7 @@ def emit(g, T, ops):
             e.wait_ge(T.sem[sem[j][0]], sem[j][1])
         if o["f"] is None:
             continue
-        ins = o["f"](e)
+        ins = o["f"](e, o["q"])
         if i in sem:
             ins.then_inc(T.sem[sem[i][0]], 16 if o.get("dma") else 1)
 
@@ -165,94 +214,88 @@ def rank_program(g, core, T, topo):
     GT, LT, AND = AluOpType.is_gt, AluOpType.is_lt, AluOpType.bitwise_and
     ACT = ActivationFunctionType
 
-    def op(q, f, r=(), w=(), **kw):
-        ops.append(dict(q=q, f=f, r=list(r), w=list(w), **kw))
+    def op(q, f, r, w, c, **kw):
+        ops.append(dict(q=q, f=f, r=list(r), w=list(w), c=c, **kw))
+        return len(ops) - 1
 
     def full(*names):
         return [(n, 0, 1 << 20) for n in names]
 
-    def move(q, out, src, r, w):
-        op(q, lambda e: e.dma_start(out, src), r, w, dma=True)
+    def el(n):
+        return 0.02 + max(64, n) * CY
 
-    def copy(q, out, in_, r, w):
-        if q == "s":
-            op("s", lambda e: e.activation(out, in_, ACT.Copy), r, w)
-        else:
-            op("v", lambda e: e.tensor_copy(out, in_), r, w)
+    def move(out, src, r, w, lat=2.0, q="y", **kw):
+        op(q, lambda e, q: e.dma_start(out, src), r, w, 0.06, dma=True, lat=lat, **kw)
 
-    def tt(out, a, b, o, r, w):
-        op("v", lambda e: e.tensor_tensor(out, a, b, o), r, w)
+    def copy(out, in_, r, w, n, q="vs", scale=None):
+        def f(e, q):
+            if q == "v":
+                return e.tensor_copy(out(), in_()) if scale is None else e.tensor_scalar(out(), in_(), scale, None, MUL)
+            return e.activation(out(), in_(), ACT.Copy) if scale is None else e.activation(out(), in_(), ACT.Copy, scale=scale)
+        op(q, f, r, w, el(n))
 
-    def ts(out, a, s1, s2, o1, o2, r, w):
+    def gather(out, win, off, r, w, n, q="vs"):
+        op(q, lambda e, q: e.tensor_copy(out, win.indirect(off)) if q == "v" else e.activation(out, win.indirect(off), ACT.Copy), r, w, 0.06 + n * GATHER * CY)
+
+    def tt(out, a, b, o, r, w, c):
+        op("v", lambda e, q: e.tensor_tensor(out, a, b, o), r, w, c)
+
+    def ts(out, a, s1, s2, o1, o2, r, w, n=64):
         if o2 is None:
-            op("v", lambda e: e.tensor_scalar(out, a, s1, None, o1), r, w)
+            op("v", lambda e, q: e.tensor_scalar(out, a, s1, None, o1), r, w, el(n))
         else:
-            op("v", lambda e: e.tensor_scalar(out, a, s1, s2, o1, o2), r, w)
+            op("v", lambda e, q: e.tensor_scalar(out, a, s1, s2, o1, o2), r, w, el(n))
 
-    def iota(out, pat, base, cm, w, small=True):
+    def iota(out, pat, base, cm, w, n, small=True, **kw):
         if small:
-            op("g", lambda e: e.iota(out, pat, base, cm, allow_small_or_imprecise_dtypes=True), (), w)
+            op("g", lambda e, q: e.iota(out, pat, base, cm, allow_small_or_imprecise_dtypes=True), (), w, 0.13 + 2 * n * CY, **kw)
         else:
-            op("g", lambda e: e.iota(out, pat, base, cm), (), w)
+            op("g", lambda e, q: e.iota(out, pat, base, cm), (), w, 0.13 + 2 * n * CY, **kw)
 
     def quant(qn, sn, a, b, src, lo, hi, r):
-        op("v", lambda e: e.quantize_mx(T[qn][:, a:b], T[sn][:, a:b], T[src][:, lo:hi]), r, [(qn, a, b)])
+        op("v", lambda e, q: e.quantize_mx(T[qn][:, a:b], T[sn][:, a:b], T[src][:, lo:hi]), r, [(qn, a, b)], 0.012 + 0.00022 * (hi - lo))
 
-    bank = [0]
+    made = [0]
 
     def mm(wn, wsn, wa, xn, xsn, a, b):
-        k = "pb%d" % bank[0]
-        bank[0] = (bank[0] + 1) % 8
-        out = T[k][:, 0:b - a]
-        op("p", lambda e: e.matmul_mx(out, T[wn][:, wa:wa + 128], T[wsn][:, wa:wa + 128], T[xn][:, a:b], T[xsn][:, a:b], True, True),
-           [(wn, wa, wa + 128), (wsn + ".load", 0, 1), (xn, a, b)], full(k))
-        return out, k
+        made[0] += 1
+        m = {"key": full("@%d" % made[0])}
+        op("p", lambda e, q: e.matmul_mx(T[m["k"]][:, 0:b - a], T[wn][:, wa:wa + 128], T[wsn][:, wa:wa + 128], T[xn][:, a:b], T[xsn][:, a:b], True, True),
+           [(wn, wa, wa + 128), (wsn + ".load", 0, 1), (xn, a, b)], m["key"], (b - a + 16) * CY, m=m)
+        m["view"] = lambda: T[m["k"]][:, 0:b - a]
+        return m
 
     def offs(name, i, lo, n):
         return T[name][:, 24 * i + lo // 16:24 * i + (lo + n) // 16]
 
-    def window(t, b):
-        if t == 0:
-            return T.xw[:], ("xw", 0, 4 * WIN)
-        return T["win%d" % t][:, WIN * b:WIN * b + WIN], ("win%d" % t, WIN * b, WIN * b + WIN)
-
-    def stage(t, b, lo, n):
-        ls, i = ("nx4", b) if t == 0 else ("pvo", t)
-        w, key = window(t, b)
-        out, off = T["P%d" % t][:, C * b + lo:C * b + lo + n], offs(ls, i, lo, n)
-        op("s", lambda e: e.activation(out, w.indirect(off), ACT.Copy), [(ls, i, i + 1), key], [("P%d" % t, C * b + lo, C * b + lo + n)])
-
-    def read(t, b, lo, n):
-        ls, i = ("pv4", b) if t == 0 else ("nxl", t)
-        w, key = window(t, b)
-        tt(T["z%d" % t][:, 4 * lo + b:4 * (lo + n):4], w.indirect(offs(ls, i, lo, n)), T["P%d" % t][:, C * b + lo:C * b + lo + n], ADD,
-           [(ls, i, i + 1), key, ("P%d" % t, C * b + lo, C * b + lo + n)], [("z%d.%d" % (t, b), lo, lo + n)])
-
-    def quant_z(t, lo, n):
+    def read(t, lo, n):
+        for b in range(4):
+            if t == 0:
+                win, key, l1, l2, i = T.xw[:], ("xw", 0, 4 * WIN), "nx4", "pv4", b
+            else:
+                win, key, l1, l2, i = T["win%d" % t][:, WIN * b:WIN * b + WIN], ("win%d" % t, WIN * b, WIN * b + WIN), "pvo", "nxl", t
+            P, k = T["P%d" % t][:, C * b + lo:C * b + lo + n], ("P%d" % t, C * b + lo, C * b + lo + n)
+            gather(P, win, offs(l1, i, lo, n), [(l1, i, i + 1), key], [k], n, "vs" if lo else STAGE_Q[b])
+            tt(T["z%d" % t][:, 4 * lo + b:4 * (lo + n):4], win.indirect(offs(l2, i, lo, n)), P, ADD, [(l2, i, i + 1), key, k],
+               [("z%d.%d" % (t, b), lo, lo + n)], 0.05 + n * GATHER * CY)
         quant("zq%d" % t, "zs%d" % t, lo, lo + n, "z%d" % t, 4 * lo, 4 * (lo + n), [("z%d.%d" % (t, b), lo, lo + n) for b in range(4)])
 
-    def layer(t, b, lo, n):
-        return mm("wq", "wsc", 128 * b, "zq%d" % t, "zs%d" % t, lo, lo + n)
-
-    def relu(q, t, b, lo, n, pk):
+    def relu(t, b, lo, n, m):
         out = T["h%d" % t][:, 4 * lo + b:4 * (lo + n):4]
-        w = [("h%d.%d" % (t, b), lo, lo + n)]
-        if q == "s":
-            op("s", lambda e: e.activation(out, pk[0], ACT.Relu, scale=0.015625), full(pk[1]), w)
-        else:
-            ts(out, pk[0], 0.0, 0.015625, MAX, MUL, full(pk[1]), w)
+        op("vs" if lo else RELU_Q[b], lambda e, q: e.activation(out, m["view"](), ACT.Relu, scale=0.015625) if q == "s" else
+           e.tensor_scalar(out, m["view"](), 0.0, 0.015625, MAX, MUL), m["key"], [("h%d.%d" % (t, b), lo, lo + n)], el(n))
 
-    def quant_h(t, lo, n):
+    def layer(t, lo, n):
+        for b in range(4):
+            relu(t, b, lo, n, mm("wq", "wsc", 128 * b, "zq%d" % t, "zs%d" % t, lo, lo + n))
         quant("hq%d" % t, "hs%d" % t, lo, lo + n, "h%d" % t, 4 * lo, 4 * (lo + n), [("h%d.%d" % (t, b), lo, lo + n) for b in range(4)])
 
-    def unpack(b, xn, xsn, lo, n):
-        return mm("eq", "es", 128 * b, xn, xsn, lo, lo + n)
+    def unpack(t, at, qn, sn, lo, n):
+        for b in range(4):
+            m, a = mm("eq", "es", 128 * b, qn, sn, lo, lo + n), WIN * b + at
+            copy(lambda a=a: T["win%d" % t][:, a:a + n], m["view"], m["key"], [("win%d" % t, a, a + n)], n, PUT_Q[b] if at == C else "vs")
 
-    def put(q, t, b, lo, n, pk):
-        a = WIN * b + lo
-        copy(q, T["win%d" % t][:, a:a + n], pk[0], full(pk[1]), [("win%d" % t, a, a + n)])
-
-    def send(t):
+    def exchange(t):
         dest = T.cores[rank ^ (1 << t)]
         rel = relays_of(core, dest, topo)
         en = hop_engines(core, rel, topo)
@@ -260,208 +303,135 @@ def rank_program(g, core, T, topo):
         hq, hs, rc, rs = T["hq%d" % t], T["hs%d" % t], T["rc%d" % t], T["rs%d" % t]
         h = G // 2
 
-        def f(e):
+        def f(e, q):
             e.remote_dma_fused([RemoteDMATransfer(dst_ids=[DstId(rid=ids[k][0], pnc=ids[k][1])], dma_engine_mask=mask_of(en[k]), remote_sem=T.sem["rarr%d" % t],
                                                   src=hq[:, h * k:h * k + h].bitcast(dt.uint8), dst=rc[:, :].bitcast(dt.uint8)) for k in range(2)], local_sem=T.sem["sent"])
             return e.remote_dma(rs[:, :], hs[:, 0:G], T.sem["rarr%d" % t], T.sem["sent"], ids[2][1], ids[2][0], mask_of(en[2]))
-        op("g", f, [("hq%d" % t, 0, G)], ())
+        i = op("g", f, [("hq%d" % t, 0, G)], (), 0.6)
+        op(None, None, (), full("gq%d" % t), 0.0, sem="garr%d" % t, val=sum(len(topo.engines(k, core)) for k in relays_of(dest, core, topo)),
+           lat=HOPS + (FIRST if t == 0 else 0.0), after=[i])
         return sum(len(x) for x in en)
 
-    def arrive(t):
-        far = T.cores[rank ^ (1 << t)]
-        op(None, None, (), full("gq%d" % t), sem="garr%d" % t, val=sum(len(topo.engines(k, core)) for k in relays_of(far, core, topo)))
-
-    def scan(dst, src, a, r):
-        op("v", lambda e: e.tensor_tensor_scan(T[dst][:], T.cc[:], T[src][:, a:a + C], 0.0, ADD, MAX), r + full("cc"), full(dst))
-
-    def signs(k):
-        o = C * k
-        tt(T.df[:, o:o + C], T.J[:, 0:C].indirect(T.pro[:, 24 * k:24 * k + 24]), T.J2[:], SUB, full("J", "J2", "pro"), [("df", k, k + 1)])
-        op("s", lambda e: e.activation(T.D[:, o:o + C], T.df[:, o:o + C], ACT.Sign), [("df", k, k + 1)], [("D", k, k + 1)])
-
-    def score(t, lo, n, pk):
-        o = C * t + lo
-        tt(T.T1[:, lo:lo + n], pk[0], T.D[:, o:o + n], MUL, full(pk[1]) + [("D", t, t + 1)], [("T1", lo, lo + n)])
-
-    def swaps(t):
-        tt(T.sw[:], T.T1[:].indirect(T.pro[:, 24 * t:24 * t + 24]), T.NT1[:], LT, full("T1", "NT1", "pro"), full("sw"))
-        scan("scs", "sw", 0, full("sw"))
-        a = slice(24 * t, 24 * t + 24)
-        tt(T.ta[:, a], T.scs[:, 15:C:16], T.dpr[:, a], MUL, full("scs", "dpr"), [("ta", t, t + 1)])
-        tt(T.tb[:, a], T.ta[:, a], T.base[:, a], ADD, [("ta", t, t + 1)] + full("base"), [("tb", t, t + 1)])
-        copy("v", T.so[:, a], T.tb[:, a], [("tb", t, t + 1)], [("so", t, t + 1)])
+    def scan(dst, src, a, r, cc="cc", n=C):
+        op("v", lambda e, q: e.tensor_tensor_scan(T[dst][:], T[cc][:], T[src][:, a:a + C], 0.0, ADD, MAX), r + full(cc), full(dst), el(n))
 
     def nxrow(t):
         return (0, C) if t == 0 else (WIN + C * (t - 1), WIN + C * t)
 
-    def swap_rows_s(t):
-        so = T.so[:, 24 * t:24 * t + 24]
-        op("s", lambda e: e.activation(T.sg[:, 0:C], T.J[:, 0:C].indirect(so), ACT.Copy), [("so", t, t + 1)] + full("J"), [("sg", 0, C)])
+    def swap_links(t):
+        a, nt = slice(24 * t, 24 * t + 24), slice(24 * t + 24, 24 * t + 48)
+        tiny = el(24)
 
-    def swap_rows_pv(t):
-        op("s", lambda e: e.activation(T.pvx[:], T.sg[:].indirect(T.pvo[:, 24 * t:24 * t + 24]), ACT.Copy), [("pvo", t, t + 1), ("sg", 0, WIN)], full("pvx"))
+        def me(*names):
+            return [(n, t, t + 1) for n in names]
 
-    def swap_rows_nx(t):
-        so = T.so[:, 24 * t:24 * t + 24]
-        a, b = nxrow(t)
-        c, d = nxrow(t + 1)
-        op("v", lambda e: e.tensor_copy(T.nxr[:, c:d], T.nxr[:, a:b].indirect(so)), [("so", t, t + 1), ("nxr", a, b)], [("nxr", c, d)])
-
-    def list_pv(t):
-        scan("scp", "pvx", 0, full("pvx"))
-        ts(T.pvo[:, 24 * t + 24:24 * t + 48], T.scp[:, 15:C:16], T.kq[:, 0:1], None, SUB, None, full("scp", "kq"), [("pvo", t + 1, t + 2)])
-
-    def list_nx(t):
-        c, d = nxrow(t + 1)
+        def nxt(*names):
+            return [(n, t + 1, t + 2) for n in names]
+        df = ("df", WIN * t, WIN * t + WIN)
+        gather(T.dnr[:], T.df[:, df[1]:df[2]], T.pvo[:, a], me("pvo") + [df], full("dnr"), C)
+        scan("scd", "dnr", 0, full("dnr"))
+        ts(T.dn[:, a], T.scd[:, 15:C:16], T.kq[:, 0:1], None, SUB, None, full("scd", "kq"), me("dn"))
+        ts(T.dk[:, a], T.dn[:, a], T.kk[:, 0:1], None, MUL, None, me("dn") + full("kk"), me("dk"))
+        tt(T.db[:, a], T.pf[:, a], T.dk[:, a], SUB, me("pf", "dk"), me("db"), tiny)
+        for lo, n in ((0, H), (H, C - H)):
+            m = mm("uq16", "us16", 0, "zq%d" % t, "zs%d" % t, lo, lo + n)
+            op("v", lambda e, q, m=m, lo=lo, n=n: e.tensor_tensor(T.T1[:, lo:lo + n], m["view"](), T.D[:, C * t + lo:C * t + lo + n], MUL),
+               m["key"] + me("D"), [("T1", lo, lo + n)], el(n))
+            copy(lambda lo=lo, n=n: T.NT1[:, lo:lo + n], lambda lo=lo, n=n: T.T1[:, lo:lo + n], [("T1", lo, lo + n)], [("NT1", lo, lo + n)], n, scale=-1.0)
+        tt(T.sw[:, 0:C], T.T1[:].indirect(T.pro[:, a]), T.NT1[:], LT, full("T1", "NT1", "pro"), [("sw", 0, C)], 0.05 + C * GATHER * CY)
+        gather(T.swp[:], T.sw[:], T.pvo[:, a], me("pvo") + [("sw", 0, WIN)], full("swp"), C)
+        scan("scq", "swp", 0, full("swp"), "ccb", C // 2)
+        tt(T.pa[:, a], T.scq[:, 15:C:16], T.dn[:, a], MUL, full("scq") + me("dn"), me("pa"), tiny)
+        tt(T.pf[:, nt], T.pa[:, a], T.db[:, a], ADD, me("pa", "db"), nxt("pf"), tiny)
+        copy(lambda: T.pvo[:, nt], lambda: T.pf[:, nt], nxt("pf"), nxt("pvo"), 24, "v")
+        scan("scs", "sw", 0, [("sw", 0, C)], "ccb", C // 2)
+        tt(T.ta[:, a], T.scs[:, 15:C:16], T.dpr[:, a], MUL, full("scs", "dpr"), me("ta"), tiny)
+        tt(T.tb[:, a], T.ta[:, a], T.base[:, a], ADD, me("ta") + full("base"), me("tb"), tiny)
+        copy(lambda: T.so[:, a], lambda: T.tb[:, a], me("tb"), me("so"), 24, "v")
+        (u, v), (c, d) = nxrow(t), nxrow(t + 1)
+        gather(T.nxr[:, c:d], T.nxr[:, u:v], T.so[:, a], me("so") + [("nxr", u, v)], [("nxr", c, d)], C)
         scan("scn", "nxr", c, [("nxr", c, d)])
-        ts(T.nxl[:, 24 * t + 24:24 * t + 48], T.scn[:, 15:C:16], T.kq[:, 0:1], None, SUB, None, full("scn", "kq"), [("nxl", t + 1, t + 2)])
+        ts(T.nxl[:, nt], T.scn[:, 15:C:16], T.kq[:, 0:1], None, SUB, None, full("scn", "kq"), nxt("nxl"))
 
-    move("y", T.nxi[:], T.nx[:], (), full("nxi"))
-    move("y", T.xw[:, 0:4 * C], T.x[:], (), [("xw", 0, 4 * C)])
-    move("y", T.xw[:, 4 * C:4 * WIN], T.gh[:], (), [("xw", 4 * C, 4 * WIN)])
-    move("y", T.pri[:], T.pr[:], (), full("pri"))
-    move("y", T.wq[:].bitcast(dt.uint8), T.wc[:], (), full("wq"))
-    move("y", T.wsc[:], T.ws[:], (), full("wsc.load"))
-    move("y", T.ut[:], T.u[:], (), full("ut"))
-    move("y", T.vt[:], T.v[:], (), full("vt"))
+    for i, (out, src, key, lat) in enumerate((
+            (T.nxi[:], T.nx[:], full("nxi"), 2.1), (T.xw[:, 0:4 * C], T.x[:], [("xw", 0, 4 * C)], 3.8), (T.xw[:, 4 * C:4 * WIN], T.gh[:], [("xw", 4 * C, 4 * WIN)], 4.8),
+            (T.pri[:], T.pr[:], full("pri"), 5.2), (T.wq[:].bitcast(dt.uint8), T.wc[:], full("wq"), 6.5), (T.wsc[:], T.ws[:], full("wsc.load"), 7.0),
+            (T.ut[:], T.u[:], full("ut"), 7.8), (T.vt[:], T.v[:], full("vt"), 8.6))):
+        move(out, src, (), key, lat, prio=1000 - i)
 
-    iota(T.pi[:], [[0, 1]], 0, 1, full("pi"), small=False)
-    iota(T.t4[:], [[1, 4]], 0, 0, full("t4"))
-    iota(T.jm[:], [[0, C // 16], [1, 16]], 0, 0, full("jm"))
-    iota(T.J[:], [[1, WIN]], 0, 0, full("J"))
-    iota(T.jo[:], [[0, R], [16, 24]], 0, 0, full("jo"))
-    iota(T.sg[:, C:WIN], [[1, G]], C, 0, [("sg", C, WIN)])
-    iota(T.uo[:], [[16, 8]], 0, 0, full("uo"), small=False)
-    op("v", lambda e: e.memset(T.ones[:], 1.0), (), full("ones"))
-    op("g", lambda e: e.affine_select(T.ee[:], T.ones[:], [[-1, 528]], AluOpType.is_equal, 0.0, 4, 4), full("ones"), full("ee"))
-    iota(T.J2[:], [[1, C]], 0, 0, full("J2"))
+    iota(T.pi[:], [[0, 1]], 0, 1, full("pi"), 1, small=False, prio=904)
+    iota(T.t4[:], [[1, 4]], 0, 0, full("t4"), 4, prio=903)
+    iota(T.jm[:], [[0, C // 16], [1, 16]], 0, 0, full("jm"), C, prio=902)
+    iota(T.J[:], [[1, WIN]], 0, 0, full("J"), WIN, prio=901)
+    iota(T.jo[:], [[0, R], [16, 24]], 0, 0, full("jo"), 72)
+    iota(T.uo[:], [[16, 8]], 0, 0, full("uo"), 8, small=False)
+    iota(T.J2[:], [[1, C]], 0, 0, full("J2"), C)
+    iota(T.sw[:, C:WIN], [[0, G]], 0, 0, [("sw", C, WIN)], G)
+    for k in range(R):
+        iota(T.df[:, WIN * k + C:WIN * k + WIN], [[0, G]], 0, 0, [("df", WIN * k + C, WIN * k + WIN)], G)
+    op("v", lambda e, q: e.memset(T.ones[:], 1.0), (), full("ones"), el(264))
+    op("g", lambda e, q: e.affine_select(T.ee[:], T.ones[:], [[-1, 528]], AluOpType.is_equal, 0.0, 4, 4), full("ones"), full("ee"), 0.17 + 1056 * CY)
     ts(T.qi[:], T.pi[:], 15, None, AND, None, full("pi"), full("qi"))
-    copy("v", T.qf[:], T.qi[:], full("qi"), full("qf"))
+    copy(lambda: T.qf[:], lambda: T.qi[:], full("qi"), full("qf"), 1, "v")
     ts(T.kq[:], T.qf[:], -float(STEP), 15.0 * STEP, MUL, ADD, full("qf"), full("kq"))
-    ts(T.cm[:], T.jm[:], T.qf[:, 0:1], float(KILL + STEP), GT, MUL, full("jm", "qf"), full("cm"))
-    ts(T.cc[:], T.cm[:], -float(KILL), None, ADD, None, full("cm"), full("cc"))
+    ts(T.kk[:], T.qf[:], -2.0, 30.0, MUL, ADD, full("qf"), full("kk"))
     ts(T.kq4[:], T.t4[:], -0.25, T.kq[:, 0:1], MUL, ADD, full("t4", "kq"), full("kq4"))
+    ts(T.cm[:], T.jm[:], T.qf[:, 0:1], float(KILL + STEP), GT, MUL, full("jm", "qf"), full("cm"), C)
+    ts(T.cc[:], T.cm[:], -float(KILL), None, ADD, None, full("cm"), full("cc"), C)
+    copy(lambda: T.ccb[:], lambda: T.cc[:], full("cc"), full("ccb"), C, "s", 2.0 / STEP)
+    for b in range(4):
+        quant("eq", "es", 128 * b, 128 * b + 128, "ee", 4 - b, 516 - b, full("ee"))
 
-    copy("v", T.nxo[:], T.nxi[:], full("nxi"), full("nxo"))
+    copy(lambda: T.nxo[:], lambda: T.nxi[:], full("nxi"), full("nxo"), 36, "v")
     for b in range(4):
         ts(T.nx4[:, 24 * b:24 * b + 24], T.nxi[:, 0:24], 4.0, float(b), MUL, ADD, full("nxi"), [("nx4", b, b + 1)])
-    op("v", lambda e: e.tensor_copy(T.pvr[:].indirect(T.nxo[:]), T.J[:]), full("J", "nxo"), full("pvr"))
-    op("s", lambda e: e.activation(T.nxr[:, 0:WIN], T.J[:].indirect(T.nxo[:]), ACT.Copy), full("J", "nxo"), [("nxr", 0, WIN)])
-    for b in range(4):
-        stage(0, b, 0, H)
+    op("v", lambda e, q: e.tensor_copy(T.pvr[:].indirect(T.nxo[:]), T.J[:]), full("J", "nxo"), full("pvr"), 0.05 + WIN * SCATTER * CY)
+    gather(T.nxr[:, 0:WIN], T.J[:], T.nxo[:], full("J", "nxo"), [("nxr", 0, WIN)], WIN, "s")
     scan("scp", "pvr", 0, full("pvr"))
     for b in range(4):
         ts(T.pv4[:, 24 * b:24 * b + 24], T.scp[:, 15:C:16], T.kq4[:, b:b + 1], 4.0, SUB, MUL, full("scp", "kq4"), [("pv4", b, b + 1)])
+    ts(T.pvo[:, 0:24], T.scp[:, 15:C:16], T.kq[:, 0:1], None, SUB, None, full("scp", "kq"), [("pvo", 0, 1)])
+    ts(T.pf[:, 0:24], T.scp[:, 15:C:16], T.kq[:, 0:1], None, SUB, None, full("scp", "kq"), [("pf", 0, 1)])
+    copy(lambda: T.pro[:], lambda: T.pri[:], full("pri"), full("pro"), 72, "v")
+    copy(lambda: T.prf[:], lambda: T.pri[:], full("pri"), full("prf"), 72, "v")
+    ts(T.joq[:], T.jo[:], T.qf[:, 0:1], None, ADD, None, full("jo", "qf"), full("joq"), 72)
+    tt(T.dpr[:], T.prf[:], T.joq[:], SUB, full("prf", "joq"), full("dpr"), el(144))
+    ts(T.kd[:], T.dpr[:], T.kk[:, 0:1], None, MUL, None, full("dpr", "kk"), full("kd"), 72)
+    tt(T.base[:], T.joq[:], T.kd[:], SUB, full("joq", "kd"), full("base"), el(144))
+    for i in range(R):
+        d, key = T.df[:, WIN * i:WIN * i + C], [("df", WIN * i, WIN * i + C)]
+        tt(d, T.J[:, 0:C].indirect(T.pro[:, 24 * i:24 * i + 24]), T.J2[:], SUB, full("J", "J2", "pro"), key, 0.05 + C * GATHER * CY)
+        op("s", lambda e, q, i=i, d=d: e.activation(T.D[:, C * i:C * i + C], d, ACT.Sign), key, [("D", i, i + 1)], el(C))
+    quant("uq", "us", 0, 128, "ut", 0, 512, full("ut"))
+    copy(lambda: T.uof[:], lambda: T.uo[:], full("uo"), full("uof"), 8, "v")
+    op("v", lambda e, q: e.tensor_copy(T.uq16[:, 0:128].bitcast(dt.uint32), T.uq[:, 0:128].bitcast(dt.uint32).indirect(T.uof[:, 0:8])),
+       full("uq", "uof"), full("uq16"), 0.05 + 128 * GATHER * CY)
+    gather(T.us16[:, 0:128], T.us[:, 0:128], T.uof[:, 0:8], full("uq", "uof"), full("us16.load"), 128)
+    quant("vq", "vs", 0, 128, "vt", 0, 512, full("vt"))
 
     sent = 0
     for t in range(R):
-        lo2, n2 = H, C - H
-        if t:
-            arrive(t - 1)
-            gk = [unpack(b, "gq%d" % (t - 1), "gs%d" % (t - 1), 0, G) for b in range(4)]
-            for b in range(4):
-                put("v", t, b, C, G, gk[b])
-            for b in range(4):
-                stage(t, b, 0, H)
-        for b in range(4):
-            read(t, b, 0, H)
-        for b in range(3):
-            stage(t, b, lo2, n2)
-        quant_z(t, 0, H)
-        k1 = [layer(t, b, 0, H) for b in range(4)]
-        if t == 0:
-            copy("v", T.pro[:], T.pri[:], full("pri"), full("pro"))
-            copy("v", T.prf[:], T.pri[:], full("pri"), full("prf"))
-            ts(T.joq[:], T.jo[:], T.qf[:, 0:1], None, ADD, None, full("jo", "qf"), full("joq"))
-            tt(T.dpr[:], T.prf[:], T.joq[:], SUB, full("prf", "joq"), full("dpr"))
-            ts(T.kd[:], T.dpr[:], T.kq[:, 0:1], None, MUL, None, full("dpr", "kq"), full("kd"))
-        relu("s", t, 0, 0, H, k1[0])
-        if t:
-            read(t, 0, lo2, n2)
-        relu("v", t, 1, 0, H, k1[1])
-        relu("s", t, 2, 0, H, k1[2])
-        relu("v", t, 3, 0, H, k1[3])
-        quant_h(t, 0, H)
-        sent += send(t)
-        if t == 0:
-            ts(T.pvo[:, 0:24], T.scp[:, 15:C:16], T.kq[:, 0:1], None, SUB, None, full("scp", "kq"), [("pvo", 0, 1)])
-            tt(T.base[:], T.joq[:], T.kd[:], SUB, full("joq", "kd"), full("base"))
-            read(0, 0, lo2, n2)
-        else:
-            ks = mm("uq16", "us16", 0, "zq%d" % t, "zs%d" % t, 0, H)
-        stage(t, 3, lo2, n2)
-        for b in range(1, 4):
-            read(t, b, lo2, n2)
-        quant_z(t, lo2, n2)
-        if t == 0:
-            quant("uq", "us", 0, 128, "ut", 0, 512, full("ut"))
-            copy("v", T.uof[:], T.uo[:], full("uo"), full("uof"))
-            op("v", lambda e: e.tensor_copy(T.uq16[:, 0:128].bitcast(dt.uint32), T.uq[:, 0:128].bitcast(dt.uint32).indirect(T.uof[:, 0:8])), full("uq", "uof"), full("uq16.q"))
-            op("v", lambda e: e.tensor_copy(T.us16[:, 0:128], T.us[:, 0:128].indirect(T.uof[:, 0:8])), full("uq", "uof", "uq16.q"), full("uq16"))
-            ks = mm("uq16", "us16", 0, "zq0", "zs0", 0, H)
-            for b in range(4):
-                quant("eq", "es", 128 * b, 128 * b + 128, "ee", 4 - b, 516 - b, full("ee"))
-        kt = mm("uq16", "us16", 0, "zq%d" % t, "zs%d" % t, lo2, C)
-        k2 = [layer(t, b, lo2, n2) for b in range(4)]
-        if t == 0:
-            signs(0)
-        score(t, 0, H, ks)
-        score(t, lo2, n2, kt)
-        op("s", lambda e: e.activation(T.NT1[:], T.T1[:], ACT.Copy, scale=-1.0), full("T1"), full("NT1"))
-        if t + 1 < R:
-            signs(t + 1)
-        ka = [unpack(b, "hq%d" % t, "hs%d" % t, 0, H) for b in range(4)]
-        for b in range(4):
-            relu("s", t, b, lo2, n2, k2[b])
-        swaps(t)
-        quant_h(t, lo2, n2)
-        put("s", t + 1, 0, 0, H, ka[0])
-        swap_rows_s(t)
-        swap_rows_pv(t)
-        put("s", t + 1, 1, 0, H, ka[1])
-        swap_rows_nx(t)
-        put("s", t + 1, 2, 0, H, ka[2])
-        kb = [unpack(b, "hq%d" % t, "hs%d" % t, lo2, n2) for b in range(4)]
-        put("v", t + 1, 3, 0, H, ka[3])
-        list_nx(t)
-        put("s", t + 1, 0, lo2, n2, kb[0])
-        put("s", t + 1, 1, lo2, n2, kb[1])
-        list_pv(t)
-        put("s", t + 1, 2, lo2, n2, kb[2])
-        put("s", t + 1, 3, lo2, n2, kb[3])
-        if t == 0:
-            quant("vq", "vs", 0, 128, "vt", 0, 512, full("vt"))
-            move("y", T.nl[:, C:WIN], T.nxr[0:128:16, C:WIN], [("nxr", C, WIN)], [("nl", C, WIN)])
-        if t == R - 1:
-            c, d = nxrow(R)
-            move("y", T.nl[:, 0:C], T.nxr[0:128:16, c:d], [("nxr", c, d)], [("nl", 0, C)])
-
-    t, cut = R, 256
-    zq, zs = T["zq%d" % R], T["zs%d" % R]
-    arrive(R - 1)
-    gk = [unpack(b, "gq%d" % (R - 1), "gs%d" % (R - 1), 0, G) for b in range(4)]
-    for b in range(4):
-        put("v", t, b, C, G, gk[b])
-    for b in range(4):
-        stage(t, b, 0, cut)
-    for b in range(4):
-        read(t, b, 0, cut)
-    quant_z(t, 0, cut)
-    k1 = mm("vq", "vs", 0, "zq%d" % R, "zs%d" % R, 0, cut)
-    move("y", T.oc[:, 0:4 * cut], zq[:, 0:cut].bitcast(dt.uint8), [("zq%d" % R, 0, cut)], [("oc", 0, cut)])
-    for b in range(4):
-        stage(t, b, cut, C - cut)
-    for b in range(4):
-        read(t, b, cut, C - cut)
-    copy("s", T.y_sb[:, 0:cut], k1[0], full(k1[1]), [("y_sb", 0, cut)])
-    move("y", T.y[:, 0:cut], T.y_sb[:, 0:cut], [("y_sb", 0, cut)], [("y", 0, cut)])
-    quant_z(t, cut, C - cut)
-    k2 = mm("vq", "vs", 0, "zq%d" % R, "zs%d" % R, cut, C)
-    move("y", T.oc[:, 4 * cut:4 * C], zq[:, cut:C].bitcast(dt.uint8), [("zq%d" % R, cut, C)], [("oc", cut, C)])
+        read(t, 0, H)
+        layer(t, 0, H)
+        sent += exchange(t)
+        read(t, H, C - H)
+        swap_links(t)
+        layer(t, H, C - H)
+        unpack(t + 1, 0, "hq%d" % t, "hs%d" % t, 0, H)
+        unpack(t + 1, H, "hq%d" % t, "hs%d" % t, H, C - H)
+        unpack(t + 1, C, "gq%d" % t, "gs%d" % t, 0, G)
+    c, d = nxrow(R)
+    move(T.nl[:, C:WIN], T.nxr[0:128:16, C:WIN], [("nxr", C, WIN)], [("nl", C, WIN)])
+    move(T.nl[:, 0:C], T.nxr[0:128:16, c:d], [("nxr", c, d)], [("nl", 0, C)])
+    zq, zs, qn = T["zq%d" % R], T["zs%d" % R], "zq%d" % R
+    for lo, n in ((0, 256), (256, 128)):
+        read(R, lo, n)
+        m = mm("vq", "vs", 0, qn, "zs%d" % R, lo, lo + n)
+        move(T.oc[:, 4 * lo:4 * (lo + n)], zq[:, lo:lo + n].bitcast(dt.uint8), [(qn, lo, lo + n)], [("oc", lo, lo + n)], 2.3)
+        copy(lambda lo=lo, n=n: T.y_sb[:, lo:lo + n], m["view"], m["key"], [("y_sb", lo, lo + n)], n)
+        move(T.y[:, lo:lo + n], T.y_sb[:, lo:lo + n], [("y_sb", lo, lo + n)], [("y", lo, lo + n)], 2.3)
     for k in range(4):
-        move("s", T.osc[4 * k:4 * k + 4, :], zs[32 * k:32 * k + 4, :], [("zq%d" % R, 0, C)], [("osc", k, k + 1)])
-    copy("v", T.y_sb[:, cut:C], k2[0], full(k2[1]), [("y_sb", cut, C)])
-    move("y", T.y[:, cut:C], T.y_sb[:, cut:C], [("y_sb", cut, C)], [("y", cut, C)])
-    op("y", None, [("oc", 0, C), ("y", 0, C), ("osc", 0, 4), ("nl", 0, WIN)], ())
-    emit(g, T, ops)
+        move(T.osc[4 * k:4 * k + 4, :], zs[32 * k:32 * k + 4, :], [(qn, 0, C)], [("osc", k, k + 1)], q="s")
+    op("y", None, [("oc", 0, C), ("y", 0, C), ("osc", 0, 4), ("nl", 0, WIN)], (), 0.0)
+    emit(g, T, schedule(ops))
     g.wait_ge(T.sem.sent, sent)

@@ -3,16 +3,29 @@ from concourse.mybir import dt, AluOpType, ActivationFunctionType
 
 C, G, R, WIN = 384, 192, 3, 576
 H = G
-STEP, KILL = 1000, 65536
+STEP, KILL = 800, 16383
 F8, BF, F32, I32, U16, U8 = "float8_e4m3fn_x4", "bfloat16", "float32", "int32", "uint16", "uint8"
-CY, GATHER, SCATTER, WAKE, HOPS, FIRST, LOOK, URGENT, EASY = 0.0011, 1.5, 3.6, 0.1, 5.0, 3.0, 0.25, 0.2, 1.0
-PUT_Q, STAGE_Q, RELU_Q = "vsvv", "ssss", "svsv"
+CY, GATHER, SCATTER, WAKE, HOPS, FIRST = 0.0011, 1.5, 3.6, 0.1, 5.0, 3.0
+ON_VECTOR = (106, 130, 134, 144, 150, 152, 165, 228, 234, 236, 238, 249, 251, 270, 293, 302, 312, 320, 322, 324)
+ORDER = [int(k) for k in """
+11 8 20 12 21 26 22 9 27 28 10 0 36 5 2 6 1 7 17 14 4 38 3 15 42 325 41 37 67 18 24 16 69 43 39 40 73 71 45 89 87 44 47 46 68 70
+74 72 75 76 77 80 81 78 79 88 50 82 83 23 93 56 62 84 91 90 94 13 63 65 19 48 64 101 92 57 29 95 104 126 122 96 52 51 102 103 120
+105 53 106 107 113 30 124 127 31 33 123 125 34 85 86 133 54 35 135 131 32 129 114 108 121 55 97 115 25 98 116 117 128 139 132 141
+49 109 134 130 143 110 137 118 136 142 58 99 100 111 145 119 147 112 149 144 138 140 146 151 150 152 148 155 156 153 154 157 159
+158 160 161 162 173 174 175 176 179 164 165 66 163 177 168 169 166 167 59 182 187 180 170 215 216 171 178 181 172 188 189 221 217
+218 183 184 190 219 220 212 210 191 192 60 185 211 206 207 193 199 213 208 209 214 225 223 227 194 200 201 222 202 186 195 196 197
+203 198 204 226 224 229 231 233 237 228 205 235 232 234 230 238 236 239 240 241 243 242 244 245 246 247 252 248 261 262 250 259 263
+260 251 61 253 249 254 255 273 256 303 307 305 265 264 266 301 274 268 275 267 306 276 269 304 277 278 270 271 292 293 257 258 298
+299 308 296 297 279 294 285 295 280 286 300 287 309 272 288 281 310 302 311 289 326 282 312 283 284 290 291 315 316 313 314 317 318
+319 320 321 322 323 324 327 328 329 330 331 332 333 334 346 347 344 340 335 337 342 345 336 343 338 339 341 348 349 356 351 354 353
+350 355 352 357""".split()]
 
 SCRATCH = {n: ("sbuf", [128, w], d) for n, w, d in (
     ("nxi", 36, I32), ("pri", 72, I32), ("xw", 4 * WIN, BF), ("ut", 512, BF), ("vt", 512, BF), ("wq", 512, F8), ("wsc", 512, U8),
-    ("J", WIN, F32), ("J2", C, F32), ("pi", 1, I32), ("qi", 1, I32), ("qf", 1, F32), ("kq", 1, F32), ("kk", 1, F32), ("t4", 4, F32), ("kq4", 4, F32),
-    ("jm", C, F32), ("cm", C, F32), ("cc", C, F32), ("ccb", C, BF), ("jo", 72, F32), ("joq", 72, F32), ("uo", 8, I32), ("uof", 8, U16),
-    ("ones", 528, BF), ("ee", 528, BF), ("eq", 512, F8), ("es", 512, U8),
+    ("J", WIN, F32), ("J2", C, F32), ("half", WIN, F32), ("pi", 1, I32), ("qi", 1, I32), ("qf", 1, F32), ("qk", 1, F32), ("kq", 1, F32), ("nkq", 1, F32),
+    ("kk", 1, F32), ("e4", 1, F32), ("t4", 4, F32), ("kq4", 4, F32),
+    ("jm", C, F32), ("cc", C, F32), ("ccb", C, BF), ("jo", 72, F32), ("joq", 72, F32), ("uo", 8, I32), ("uof", 8, U16),
+    ("ab", 528, BF), ("ee", 528, BF), ("eq", 512, F8), ("es", 512, U8),
     ("uq", 128, F8), ("us", 128, U8), ("uq16", 128, F8), ("us16", 128, U8), ("vq", 128, F8), ("vs", 128, U8),
     ("nxo", 36, U16), ("nx4", 96, U16), ("pv4", 96, U16), ("pvo", 96, U16), ("nxl", 96, U16), ("pro", 72, U16), ("so", 72, U16),
     ("prf", 72, F32), ("dpr", 72, F32), ("kd", 72, F32), ("base", 72, F32), ("ta", 72, F32), ("tb", 72, F32),
@@ -28,7 +41,7 @@ for _t in range(R + 1):
 for _b in range(8):
     SCRATCH["pb%d" % _b] = ("psum", [128, 512], F32)
 
-SEMAPHORES = (["c%d" % i for i in range(100)] + ["d%d" % i for i in range(30)]
+SEMAPHORES = (["c%d" % i for i in range(60)] + ["d%d" % i for i in range(30)]
               + ["rarr%d" % t for t in range(R)] + ["garr%d" % t for t in range(R)] + ["sent"])
 
 
@@ -97,68 +110,33 @@ def dependencies(ops):
     return out
 
 
-def schedule(ops):
-    deps = dependencies(ops)
-    n = len(ops)
-    tail, readers = [0.0] * n, {}
-    for i in range(n - 1, -1, -1):
-        o = ops[i]
-        tail[i] += o["c"] + o.get("lat", 0.0)
-        for j in deps[i]:
-            tail[j] = max(tail[j], tail[i] + WAKE)
+def arrange(ops):
+    at = {k: i for i, k in enumerate(ORDER)}
+    assert sorted(at) == list(range(len(ops)))
+    assert all(at[j] < at[i] for i, d in enumerate(dependencies(ops)) for j in d)
+    assert all(ops[i]["q"] == "vs" for i in ON_VECTOR)
+    readers = {}
+    for i, o in enumerate(ops):
+        if o["q"] == "vs":
+            o["q"] = "v" if i in ON_VECTOR else "s"
         for k, lo, hi in o["r"]:
             if k[0] == "@":
-                readers.setdefault(k, []).append(i)
-    prio = [o.get("prio", tail[i]) for i, o in enumerate(ops)]
-    free, end, start = {q: 0.0 for q in "gvspy"}, {}, {}
-    banks, todo = [None] * 8, list(range(n))
-
-    def bank_free(k):
-        return 0.0 if k is None else max(end[j] + WAKE for j in readers[k]) if all(j in end for j in readers[k]) else None
-    while todo:
-        cand, ready, arrived = {}, {}, None
-        for i in todo:
-            if any(j not in end for j in deps[i]):
-                continue
-            o = ops[i]
-            ready[i] = max([end[j] + WAKE for j in deps[i]] + [0.0])
-            if o["q"] is None:
-                start[i], end[i], arrived = ready[i], ready[i] + o.get("lat", 0.0), i
-                break
-            if "m" in o:
-                b = [x for x in map(bank_free, banks) if x is not None]
-                if not b:
-                    continue
-                ready[i] = max(ready[i], min(b))
-            for q in o["q"]:
-                cand.setdefault(q, []).append((max(free[q], ready[i]), i))
-        if arrived is not None:
-            todo.remove(arrived)
-            continue
-        own = max([prio[i] for s, i in cand.get("v", ()) if ops[i]["q"] == "v"] + [0.0])
-        cand["v"] = [(s, i) for s, i in cand.get("v", ()) if ops[i]["q"] == "v" or max(free["s"], ready[i]) > s + (URGENT if prio[i] > own else EASY)]
-        pick = None
-        for q, l in cand.items():
-            if l:
-                t0 = min(l)[0]
-                p, s, i = max((prio[i], -s, -i) for s, i in l if s <= t0 + LOOK)
-                if pick is None or (s, -p) > pick[:2]:
-                    pick = (s, -p, -i, q)
-        s, i, q = -pick[0], pick[2], pick[3]
+                readers.setdefault(k, set()).add(i)
+    free, names = ["pb%d" % b for b in range(8)], {}
+    for i in ORDER:
         o = ops[i]
         if "m" in o:
-            x = min((bank_free(k), x) for x, k in enumerate(banks) if bank_free(k) is not None)[1]
-            banks[x] = o["w"][0][0]
-            o["m"]["k"] = "pb%d" % x
-        o["q"], start[i], free[q] = q, s, s + o["c"]
-        end[i] = free[q] + o.get("lat", 0.0)
-        todo.remove(i)
-    names = {o["w"][0][0]: o["m"]["k"] for o in ops if "m" in o}
+            names[o["w"][0][0]] = o["m"]["k"] = free.pop(0)
+        for k, lo, hi in o["r"]:
+            if k[0] == "@":
+                readers[k].discard(i)
+                if not readers[k]:
+                    free.append(names[k])
     for o in ops:
         o["after"] = ()
         for a in "rw":
             o[a] = [(names.get(k, k), lo, hi) for k, lo, hi in o[a]]
-    return [ops[i] for i in sorted(range(n), key=lambda i: (start[i], i))]
+    return [ops[i] for i in ORDER]
 
 
 def emit(g, T, ops):
@@ -210,8 +188,8 @@ def rank_program(g, core, T, topo):
     if rank is None:
         return relay_program(g, core, T, topo)
     ops = []
-    ADD, SUB, MUL, MAX = AluOpType.add, AluOpType.subtract, AluOpType.mult, AluOpType.max
-    GT, LT, AND = AluOpType.is_gt, AluOpType.is_lt, AluOpType.bitwise_and
+    ADD, SUB, MUL, MAX, MIN = AluOpType.add, AluOpType.subtract, AluOpType.mult, AluOpType.max, AluOpType.min
+    LT, AND = AluOpType.is_lt, AluOpType.bitwise_and
     ACT = ActivationFunctionType
 
     def op(q, f, r, w, c, **kw):
@@ -224,8 +202,8 @@ def rank_program(g, core, T, topo):
     def el(n):
         return 0.02 + max(64, n) * CY
 
-    def move(out, src, r, w, lat=2.0, q="y", **kw):
-        op(q, lambda e, q: e.dma_start(out, src), r, w, 0.06, dma=True, lat=lat, **kw)
+    def move(out, src, r, w, lat=2.0, q="y"):
+        op(q, lambda e, q: e.dma_start(out, src), r, w, 0.06, dma=True, lat=lat)
 
     def copy(out, in_, r, w, n, q="vs", scale=None):
         def f(e, q):
@@ -246,11 +224,19 @@ def rank_program(g, core, T, topo):
         else:
             op("v", lambda e, q: e.tensor_scalar(out, a, s1, s2, o1, o2), r, w, el(n))
 
-    def iota(out, pat, base, cm, w, n, small=True, **kw):
+    def minus(out, a, col, neg, r, w, n=64):
+        op("vs", lambda e, q: e.tensor_scalar(out, a, T[col][:, 0:1], None, SUB) if q == "v" else
+           e.activation(out, a, ACT.Identity, bias=T[neg][:, 0:1]), r + full(col, neg), w, el(n))
+
+    def times(out, a, col, r, w, n=64):
+        op("vs", lambda e, q: e.tensor_scalar(out, a, T[col][:, 0:1], None, MUL) if q == "v" else
+           e.activation(out, a, ACT.Identity, scale=T[col][:, 0:1]), r + full(col), w, el(n))
+
+    def iota(out, pat, base, cm, w, n, small=True):
         if small:
-            op("g", lambda e, q: e.iota(out, pat, base, cm, allow_small_or_imprecise_dtypes=True), (), w, 0.13 + 2 * n * CY, **kw)
+            op("g", lambda e, q: e.iota(out, pat, base, cm, allow_small_or_imprecise_dtypes=True), (), w, 0.13 + 2 * n * CY)
         else:
-            op("g", lambda e, q: e.iota(out, pat, base, cm), (), w, 0.13 + 2 * n * CY, **kw)
+            op("g", lambda e, q: e.iota(out, pat, base, cm), (), w, 0.13 + 2 * n * CY)
 
     def quant(qn, sn, a, b, src, lo, hi, r):
         op("v", lambda e, q: e.quantize_mx(T[qn][:, a:b], T[sn][:, a:b], T[src][:, lo:hi]), r, [(qn, a, b)], 0.012 + 0.00022 * (hi - lo))
@@ -275,14 +261,14 @@ def rank_program(g, core, T, topo):
             else:
                 win, key, l1, l2, i = T["win%d" % t][:, WIN * b:WIN * b + WIN], ("win%d" % t, WIN * b, WIN * b + WIN), "pvo", "nxl", t
             P, k = T["P%d" % t][:, C * b + lo:C * b + lo + n], ("P%d" % t, C * b + lo, C * b + lo + n)
-            gather(P, win, offs(l1, i, lo, n), [(l1, i, i + 1), key], [k], n, "vs" if lo else STAGE_Q[b])
+            gather(P, win, offs(l1, i, lo, n), [(l1, i, i + 1), key], [k], n)
             tt(T["z%d" % t][:, 4 * lo + b:4 * (lo + n):4], win.indirect(offs(l2, i, lo, n)), P, ADD, [(l2, i, i + 1), key, k],
                [("z%d.%d" % (t, b), lo, lo + n)], 0.05 + n * GATHER * CY)
         quant("zq%d" % t, "zs%d" % t, lo, lo + n, "z%d" % t, 4 * lo, 4 * (lo + n), [("z%d.%d" % (t, b), lo, lo + n) for b in range(4)])
 
     def relu(t, b, lo, n, m):
         out = T["h%d" % t][:, 4 * lo + b:4 * (lo + n):4]
-        op("vs" if lo else RELU_Q[b], lambda e, q: e.activation(out, m["view"](), ACT.Relu, scale=0.015625) if q == "s" else
+        op("vs", lambda e, q: e.activation(out, m["view"](), ACT.Relu, scale=0.015625) if q == "s" else
            e.tensor_scalar(out, m["view"](), 0.0, 0.015625, MAX, MUL), m["key"], [("h%d.%d" % (t, b), lo, lo + n)], el(n))
 
     def layer(t, lo, n):
@@ -293,7 +279,7 @@ def rank_program(g, core, T, topo):
     def unpack(t, at, qn, sn, lo, n):
         for b in range(4):
             m, a = mm("eq", "es", 128 * b, qn, sn, lo, lo + n), WIN * b + at
-            copy(lambda a=a: T["win%d" % t][:, a:a + n], m["view"], m["key"], [("win%d" % t, a, a + n)], n, PUT_Q[b] if at == C else "vs")
+            copy(lambda a=a: T["win%d" % t][:, a:a + n], m["view"], m["key"], [("win%d" % t, a, a + n)], n)
 
     def exchange(t):
         dest = T.cores[rank ^ (1 << t)]
@@ -330,8 +316,8 @@ def rank_program(g, core, T, topo):
         df = ("df", WIN * t, WIN * t + WIN)
         gather(T.dnr[:], T.df[:, df[1]:df[2]], T.pvo[:, a], me("pvo") + [df], full("dnr"), C)
         scan("scd", "dnr", 0, full("dnr"))
-        ts(T.dn[:, a], T.scd[:, 15:C:16], T.kq[:, 0:1], None, SUB, None, full("scd", "kq"), me("dn"))
-        ts(T.dk[:, a], T.dn[:, a], T.kk[:, 0:1], None, MUL, None, me("dn") + full("kk"), me("dk"))
+        minus(T.dn[:, a], T.scd[:, 15:C:16], "kq", "nkq", full("scd"), me("dn"))
+        times(T.dk[:, a], T.dn[:, a], "kk", me("dn"), me("dk"))
         tt(T.db[:, a], T.pf[:, a], T.dk[:, a], SUB, me("pf", "dk"), me("db"), tiny)
         for lo, n in ((0, H), (H, C - H)):
             m = mm("uq16", "us16", 0, "zq%d" % t, "zs%d" % t, lo, lo + n)
@@ -353,32 +339,35 @@ def rank_program(g, core, T, topo):
         scan("scn", "nxr", c, [("nxr", c, d)])
         ts(T.nxl[:, nt], T.scn[:, 15:C:16], T.kq[:, 0:1], None, SUB, None, full("scn", "kq"), nxt("nxl"))
 
-    for i, (out, src, key, lat) in enumerate((
+    for out, src, key, lat in (
             (T.nxi[:], T.nx[:], full("nxi"), 2.1), (T.xw[:, 0:4 * C], T.x[:], [("xw", 0, 4 * C)], 3.8), (T.xw[:, 4 * C:4 * WIN], T.gh[:], [("xw", 4 * C, 4 * WIN)], 4.8),
             (T.pri[:], T.pr[:], full("pri"), 5.2), (T.wq[:].bitcast(dt.uint8), T.wc[:], full("wq"), 6.5), (T.wsc[:], T.ws[:], full("wsc.load"), 7.0),
-            (T.ut[:], T.u[:], full("ut"), 7.8), (T.vt[:], T.v[:], full("vt"), 8.6))):
-        move(out, src, (), key, lat, prio=1000 - i)
+            (T.ut[:], T.u[:], full("ut"), 7.8), (T.vt[:], T.v[:], full("vt"), 8.6)):
+        move(out, src, (), key, lat)
 
-    iota(T.pi[:], [[0, 1]], 0, 1, full("pi"), 1, small=False, prio=904)
-    iota(T.t4[:], [[1, 4]], 0, 0, full("t4"), 4, prio=903)
-    iota(T.jm[:], [[0, C // 16], [1, 16]], 0, 0, full("jm"), C, prio=902)
-    iota(T.J[:], [[1, WIN]], 0, 0, full("J"), WIN, prio=901)
+    iota(T.pi[:], [[0, 1]], 0, 1, full("pi"), 1, small=False)
+    iota(T.jm[:], [[0, C // 16], [2 * KILL, 16]], 0, 0, full("jm"), C)
+    iota(T.t4[:], [[1, 4]], 0, 0, full("t4"), 4)
+    op("v", lambda e, q: e.memset(T.half[:], 0.5), (), full("half"), el(WIN))
+    op("v", lambda e, q: e.tensor_tensor_scan(T.J[:], T.half[:], T.half[:], -1.0, ADD, ADD), full("half"), full("J"), el(WIN))
     iota(T.jo[:], [[0, R], [16, 24]], 0, 0, full("jo"), 72)
     iota(T.uo[:], [[16, 8]], 0, 0, full("uo"), 8, small=False)
     iota(T.J2[:], [[1, C]], 0, 0, full("J2"), C)
     iota(T.sw[:, C:WIN], [[0, G]], 0, 0, [("sw", C, WIN)], G)
     for k in range(R):
         iota(T.df[:, WIN * k + C:WIN * k + WIN], [[0, G]], 0, 0, [("df", WIN * k + C, WIN * k + WIN)], G)
-    op("v", lambda e, q: e.memset(T.ones[:], 1.0), (), full("ones"), el(264))
-    op("g", lambda e, q: e.affine_select(T.ee[:], T.ones[:], [[-1, 528]], AluOpType.is_equal, 0.0, 4, 4), full("ones"), full("ee"), 0.17 + 1056 * CY)
     ts(T.qi[:], T.pi[:], 15, None, AND, None, full("pi"), full("qi"))
     copy(lambda: T.qf[:], lambda: T.qi[:], full("qi"), full("qf"), 1, "v")
     ts(T.kq[:], T.qf[:], -float(STEP), 15.0 * STEP, MUL, ADD, full("qf"), full("kq"))
     ts(T.kk[:], T.qf[:], -2.0, 30.0, MUL, ADD, full("qf"), full("kk"))
     ts(T.kq4[:], T.t4[:], -0.25, T.kq[:, 0:1], MUL, ADD, full("t4", "kq"), full("kq4"))
-    ts(T.cm[:], T.jm[:], T.qf[:, 0:1], float(KILL + STEP), GT, MUL, full("jm", "qf"), full("cm"), C)
-    ts(T.cc[:], T.cm[:], -float(KILL), None, ADD, None, full("cm"), full("cc"), C)
+    ts(T.nkq[:], T.kq[:], -1.0, None, MUL, None, full("kq"), full("nkq"))
+    ts(T.qk[:], T.qf[:], 2.0 * KILL, float(KILL), MUL, ADD, full("qf"), full("qk"))
+    ts(T.cc[:], T.jm[:], T.qk[:, 0:1], float(STEP), SUB, MIN, full("jm", "qk"), full("cc"), C)
     copy(lambda: T.ccb[:], lambda: T.cc[:], full("cc"), full("ccb"), C, "s", 2.0 / STEP)
+    ts(T.e4[:], T.pi[:], -4.0, -4.0, MUL, ADD, full("pi"), full("e4"))
+    op("s", lambda e, q: e.activation(T.ab[:], T.J[:, 0:528], ACT.Abs, bias=T.e4[:, 0:1]), full("J", "e4"), full("ab"), el(528))
+    op("s", lambda e, q: e.activation(T.ee[:], T.ab[:], ACT.Relu, bias=1.0, scale=-1.0), full("ab"), full("ee"), el(528))
     for b in range(4):
         quant("eq", "es", 128 * b, 128 * b + 128, "ee", 4 - b, 516 - b, full("ee"))
 
@@ -391,12 +380,12 @@ def rank_program(g, core, T, topo):
     for b in range(4):
         ts(T.pv4[:, 24 * b:24 * b + 24], T.scp[:, 15:C:16], T.kq4[:, b:b + 1], 4.0, SUB, MUL, full("scp", "kq4"), [("pv4", b, b + 1)])
     ts(T.pvo[:, 0:24], T.scp[:, 15:C:16], T.kq[:, 0:1], None, SUB, None, full("scp", "kq"), [("pvo", 0, 1)])
-    ts(T.pf[:, 0:24], T.scp[:, 15:C:16], T.kq[:, 0:1], None, SUB, None, full("scp", "kq"), [("pf", 0, 1)])
+    minus(T.pf[:, 0:24], T.scp[:, 15:C:16], "kq", "nkq", full("scp"), [("pf", 0, 1)])
     copy(lambda: T.pro[:], lambda: T.pri[:], full("pri"), full("pro"), 72, "v")
     copy(lambda: T.prf[:], lambda: T.pri[:], full("pri"), full("prf"), 72, "v")
     ts(T.joq[:], T.jo[:], T.qf[:, 0:1], None, ADD, None, full("jo", "qf"), full("joq"), 72)
     tt(T.dpr[:], T.prf[:], T.joq[:], SUB, full("prf", "joq"), full("dpr"), el(144))
-    ts(T.kd[:], T.dpr[:], T.kk[:, 0:1], None, MUL, None, full("dpr", "kk"), full("kd"), 72)
+    times(T.kd[:], T.dpr[:], "kk", full("dpr"), full("kd"), 72)
     tt(T.base[:], T.joq[:], T.kd[:], SUB, full("joq", "kd"), full("base"), el(144))
     for i in range(R):
         d, key = T.df[:, WIN * i:WIN * i + C], [("df", WIN * i, WIN * i + C)]
@@ -433,5 +422,5 @@ def rank_program(g, core, T, topo):
     for k in range(4):
         move(T.osc[4 * k:4 * k + 4, :], zs[32 * k:32 * k + 4, :], [(qn, 0, C)], [("osc", k, k + 1)], q="s")
     op("y", None, [("oc", 0, C), ("y", 0, C), ("osc", 0, 4), ("nl", 0, WIN)], (), 0.0)
-    emit(g, T, schedule(ops))
+    emit(g, T, arrange(ops))
     g.wait_ge(T.sem.sent, sent)

from concourse.bass import DstId, RemoteDMATransfer
from concourse.mybir import dt, AluOpType, ActivationFunctionType

C, G, R, WIN = 384, 192, 3, 576
H = G
STEP, KILL = 800, 16383
F8, BF, F32, I32, U16, U8 = "float8_e4m3fn_x4", "bfloat16", "float32", "int32", "uint16", "uint8"
CY, GATHER, SCATTER, WAKE, HOPS, FIRST = 0.0011, 1.5, 3.6, 0.1, 5.0, 3.0
ON_VECTOR = (106, 130, 134, 144, 150, 152, 165, 228, 234, 236, 238, 249, 251, 270, 293, 302, 312, 320, 322, 324)
ORDER = [int(k) for k in """
11 8 20 12 21 26 22 9 27 28 10 0 36 5 2 6 1 7 17 14 4 38 3 15 42 325 41 37 67 18 24 16 69 43 39 40 73 71 45 89 87 44 47 46 68 70
74 72 75 76 77 80 81 78 79 88 50 82 83 23 93 56 62 84 91 90 94 13 63 65 19 48 64 101 92 57 29 95 104 126 122 96 52 51 102 103 120
105 53 106 107 113 30 124 127 31 33 123 125 34 85 86 133 54 35 135 131 32 129 114 108 121 55 97 115 25 98 116 117 128 139 132 141
49 109 134 130 143 110 137 118 136 142 58 99 100 111 145 119 147 112 149 144 138 140 146 151 150 152 148 155 156 153 154 157 159
158 160 161 162 173 174 175 176 179 164 165 66 163 177 168 169 166 167 59 182 187 180 170 215 216 171 178 181 172 188 189 221 217
218 183 184 190 219 220 212 210 191 192 60 185 211 206 207 193 199 213 208 209 214 225 223 227 194 200 201 222 202 186 195 196 197
203 198 204 226 224 229 231 233 237 228 205 235 232 234 230 238 236 239 240 241 243 242 244 245 246 247 252 248 261 262 250 259 263
260 251 61 253 249 254 255 273 256 303 307 305 265 264 266 301 274 268 275 267 306 276 269 304 277 278 270 271 292 293 257 258 298
299 308 296 297 279 294 285 295 280 286 300 287 309 272 288 281 310 302 311 289 326 282 312 283 284 290 291 315 316 313 314 317 318
319 320 321 322 323 324 327 328 329 330 331 332 333 334 346 347 344 340 335 337 342 345 336 343 338 339 341 348 349 356 351 354 353
350 355 352 357""".split()]

SCRATCH = {n: ("sbuf", [128, w], d) for n, w, d in (
    ("nxi", 36, I32), ("pri", 72, I32), ("xw", 4 * WIN, BF), ("ut", 512, BF), ("vt", 512, BF), ("wq", 512, F8), ("wsc", 512, U8),
    ("J", WIN, F32), ("J2", C, F32), ("half", WIN, F32), ("pi", 1, I32), ("qi", 1, I32), ("qf", 1, F32), ("qk", 1, F32), ("kq", 1, F32), ("nkq", 1, F32),
    ("kk", 1, F32), ("e4", 1, F32), ("t4", 4, F32), ("kq4", 4, F32),
    ("jm", C, F32), ("cc", C, F32), ("ccb", C, BF), ("jo", 72, F32), ("joq", 72, F32), ("uo", 8, I32), ("uof", 8, U16),
    ("ab", 528, BF), ("ee", 528, BF), ("eq", 512, F8), ("es", 512, U8),
    ("uq", 128, F8), ("us", 128, U8), ("uq16", 128, F8), ("us16", 128, U8), ("vq", 128, F8), ("vs", 128, U8),
    ("nxo", 36, U16), ("nx4", 96, U16), ("pv4", 96, U16), ("pvo", 96, U16), ("nxl", 96, U16), ("pro", 72, U16), ("so", 72, U16),
    ("prf", 72, F32), ("dpr", 72, F32), ("kd", 72, F32), ("base", 72, F32), ("ta", 72, F32), ("tb", 72, F32),
    ("dn", 72, F32), ("dk", 72, F32), ("db", 72, F32), ("pa", 72, F32), ("pf", 96, F32),
    ("nxr", WIN + 3 * C, F32), ("pvr", WIN, F32), ("df", 3 * WIN, F32), ("D", 3 * C, F32), ("T1", C, F32), ("NT1", C, F32),
    ("sw", WIN, BF), ("swp", C, BF), ("scq", C, BF), ("scs", C, BF), ("scn", C, F32), ("scp", C, F32), ("dnr", C, F32), ("scd", C, F32), ("y_sb", C, F32))}
for _t in range(R + 1):
    SCRATCH.update({"%s%d" % (n, _t): ("sbuf", [128, w], d) for n, w, d in (("P", 4 * C, BF), ("z", 4 * C, BF), ("zq", C, F8), ("zs", C, U8))})
    if _t < R:
        SCRATCH["win%d" % (_t + 1)] = ("sbuf", [128, 4 * WIN], BF)
        SCRATCH.update({"%s%d" % (n, _t): ("sbuf", [128, w], d) for n, w, d in (
            ("h", 4 * C, BF), ("hq", C, F8), ("hs", C, U8), ("rc", G // 2, F8), ("rs", G, U8), ("gq", G, F8), ("gs", G, U8))})
for _b in range(8):
    SCRATCH["pb%d" % _b] = ("psum", [128, 512], F32)

SEMAPHORES = (["c%d" % i for i in range(60)] + ["d%d" % i for i in range(30)]
              + ["rarr%d" % t for t in range(R)] + ["garr%d" % t for t in range(R)] + ["sent"])


def mask_of(engines):
    m = 0
    for e in engines:
        m |= 1 << e
    return m


def relays_of(core, dest, topo):
    c = [k for k in topo.cores_of(core) if k != core and topo.may_write(k, dest)]
    near = [k for k in c if topo.die(k) == topo.die(core)]
    far = [k for k in c if topo.die(k) != topo.die(core)]
    return [near[0], far[0], near[1]]


def hop_engines(core, relays, topo):
    e0, e1, e2 = (topo.engines(core, k) for k in relays)
    h = len(e0) // 2
    return [e0[:h], e1[h:], e2]


def relay_program(g, core, T, topo):
    mine = [c for c in T.cores if c in topo.cores_of(core)]
    if not mine:
        return
    src = mine[0]
    r = T.rank_of(src)
    total = 0
    for t in range(R):
        dest = T.cores[r ^ (1 << t)]
        rel = relays_of(src, dest, topo)
        if core not in rel:
            continue
        k = rel.index(core)
        rid, pid = topo.addr(dest, core)
        if k < 2:
            a, b = k * (G // 2), (k + 1) * (G // 2)
            out, inn = T["gq%d" % t][:, a:b].bitcast(dt.uint8), T["rc%d" % t][:, :].bitcast(dt.uint8)
        else:
            out, inn = T["gs%d" % t][:, :], T["rs%d" % t][:, :]
        g.wait_ge(T.sem["rarr%d" % t], len(hop_engines(src, rel, topo)[k]))
        g.remote_dma(out, inn, T.sem["garr%d" % t], T.sem["sent"], pid, rid, topo.mask(core, dest))
        total += len(topo.engines(core, dest))
    if total:
        g.wait_ge(T.sem["sent"], total)


def dependencies(ops):
    hist, out = {}, []
    for i, o in enumerate(ops):
        deps = set(o.get("after", ()))
        for k, lo, hi in o["r"]:
            deps |= {j for (a, b, j, wr) in hist.get(k, ()) if wr and a < hi and lo < b}
        for k, lo, hi in o["w"]:
            deps |= {j for (a, b, j, wr) in hist.get(k, ()) if a < hi and lo < b}
        for k, lo, hi in o["w"]:
            lst = hist.setdefault(k, [])
            lst[:] = [e for e in lst if not (lo <= e[0] and e[1] <= hi)]
            lst.append((lo, hi, i, True))
        for k, lo, hi in o["r"]:
            hist.setdefault(k, []).append((lo, hi, i, False))
        deps.discard(i)
        out.append(deps)
    return out


def arrange(ops):
    at = {k: i for i, k in enumerate(ORDER)}
    assert sorted(at) == list(range(len(ops)))
    assert all(at[j] < at[i] for i, d in enumerate(dependencies(ops)) for j in d)
    assert all(ops[i]["q"] == "vs" for i in ON_VECTOR)
    readers = {}
    for i, o in enumerate(ops):
        if o["q"] == "vs":
            o["q"] = "v" if i in ON_VECTOR else "s"
        for k, lo, hi in o["r"]:
            if k[0] == "@":
                readers.setdefault(k, set()).add(i)
    free, names = ["pb%d" % b for b in range(8)], {}
    for i in ORDER:
        o = ops[i]
        if "m" in o:
            names[o["w"][0][0]] = o["m"]["k"] = free.pop(0)
        for k, lo, hi in o["r"]:
            if k[0] == "@":
                readers[k].discard(i)
                if not readers[k]:
                    free.append(names[k])
    for o in ops:
        o["after"] = ()
        for a in "rw":
            o[a] = [(names.get(k, k), lo, hi) for k, lo, hi in o[a]]
    return [ops[i] for i in ORDER]


def emit(g, T, ops):
    queues = {"g": g, "v": g.vector, "s": g.scalar, "p": g.tensor, "y": g.sync}
    know, at, need, used = {q: set() for q in queues}, [], [], set()
    for i, (o, deps) in enumerate(zip(ops, dependencies(ops))):
        w = []
        if o["q"] is None:
            at.append(set())
        else:
            kq = know[o["q"]]
            for j in sorted(deps, reverse=True):
                if j not in kq:
                    w.append(j)
                    used.add(j)
                    kq.add(j)
                    kq |= at[j]
            at.append(set(kq))
        need.append(w)
    last, count, sem = {}, {}, {}
    for i, o in enumerate(ops):
        if i not in used:
            continue
        if o["q"] is None:
            sem[i] = (o["sem"], o["val"])
            continue
        kind, n = ("d", 16) if o.get("dma") else ("c", 1)
        k = 0
        while (kind, k) in last and last[(kind, k)] not in at[i]:
            k += 1
        last[(kind, k)] = i
        count[(kind, k)] = count.get((kind, k), 0) + n
        sem[i] = ("%s%d" % (kind, k), count[(kind, k)])
    for i, o in enumerate(ops):
        if o["q"] is None:
            continue
        e = queues[o["q"]]
        for j in need[i]:
            e.wait_ge(T.sem[sem[j][0]], sem[j][1])
        if o["f"] is None:
            continue
        ins = o["f"](e, o["q"])
        if i in sem:
            ins.then_inc(T.sem[sem[i][0]], 16 if o.get("dma") else 1)


def rank_program(g, core, T, topo):
    rank = T.rank_of(core)
    if rank is None:
        return relay_program(g, core, T, topo)
    ops = []
    ADD, SUB, MUL, MAX, MIN = AluOpType.add, AluOpType.subtract, AluOpType.mult, AluOpType.max, AluOpType.min
    LT, AND = AluOpType.is_lt, AluOpType.bitwise_and
    ACT = ActivationFunctionType

    def op(q, f, r, w, c, **kw):
        ops.append(dict(q=q, f=f, r=list(r), w=list(w), c=c, **kw))
        return len(ops) - 1

    def full(*names):
        return [(n, 0, 1 << 20) for n in names]

    def el(n):
        return 0.02 + max(64, n) * CY

    def move(out, src, r, w, lat=2.0, q="y"):
        op(q, lambda e, q: e.dma_start(out, src), r, w, 0.06, dma=True, lat=lat)

    def copy(out, in_, r, w, n, q="vs", scale=None):
        def f(e, q):
            if q == "v":
                return e.tensor_copy(out(), in_()) if scale is None else e.tensor_scalar(out(), in_(), scale, None, MUL)
            return e.activation(out(), in_(), ACT.Copy) if scale is None else e.activation(out(), in_(), ACT.Copy, scale=scale)
        op(q, f, r, w, el(n))

    def gather(out, win, off, r, w, n, q="vs"):
        op(q, lambda e, q: e.tensor_copy(out, win.indirect(off)) if q == "v" else e.activation(out, win.indirect(off), ACT.Copy), r, w, 0.06 + n * GATHER * CY)

    def tt(out, a, b, o, r, w, c):
        op("v", lambda e, q: e.tensor_tensor(out, a, b, o), r, w, c)

    def ts(out, a, s1, s2, o1, o2, r, w, n=64):
        if o2 is None:
            op("v", lambda e, q: e.tensor_scalar(out, a, s1, None, o1), r, w, el(n))
        else:
            op("v", lambda e, q: e.tensor_scalar(out, a, s1, s2, o1, o2), r, w, el(n))

    def minus(out, a, col, neg, r, w, n=64):
        op("vs", lambda e, q: e.tensor_scalar(out, a, T[col][:, 0:1], None, SUB) if q == "v" else
           e.activation(out, a, ACT.Identity, bias=T[neg][:, 0:1]), r + full(col, neg), w, el(n))

    def times(out, a, col, r, w, n=64):
        op("vs", lambda e, q: e.tensor_scalar(out, a, T[col][:, 0:1], None, MUL) if q == "v" else
           e.activation(out, a, ACT.Identity, scale=T[col][:, 0:1]), r + full(col), w, el(n))

    def iota(out, pat, base, cm, w, n, small=True):
        if small:
            op("g", lambda e, q: e.iota(out, pat, base, cm, allow_small_or_imprecise_dtypes=True), (), w, 0.13 + 2 * n * CY)
        else:
            op("g", lambda e, q: e.iota(out, pat, base, cm), (), w, 0.13 + 2 * n * CY)

    def quant(qn, sn, a, b, src, lo, hi, r):
        op("v", lambda e, q: e.quantize_mx(T[qn][:, a:b], T[sn][:, a:b], T[src][:, lo:hi]), r, [(qn, a, b)], 0.012 + 0.00022 * (hi - lo))

    made = [0]

    def mm(wn, wsn, wa, xn, xsn, a, b):
        made[0] += 1
        m = {"key": full("@%d" % made[0])}
        op("p", lambda e, q: e.matmul_mx(T[m["k"]][:, 0:b - a], T[wn][:, wa:wa + 128], T[wsn][:, wa:wa + 128], T[xn][:, a:b], T[xsn][:, a:b], True, True),
           [(wn, wa, wa + 128), (wsn + ".load", 0, 1), (xn, a, b)], m["key"], (b - a + 16) * CY, m=m)
        m["view"] = lambda: T[m["k"]][:, 0:b - a]
        return m

    def offs(name, i, lo, n):
        return T[name][:, 24 * i + lo // 16:24 * i + (lo + n) // 16]

    def read(t, lo, n):
        for b in range(4):
            if t == 0:
                win, key, l1, l2, i = T.xw[:], ("xw", 0, 4 * WIN), "nx4", "pv4", b
            else:
                win, key, l1, l2, i = T["win%d" % t][:, WIN * b:WIN * b + WIN], ("win%d" % t, WIN * b, WIN * b + WIN), "pvo", "nxl", t
            P, k = T["P%d" % t][:, C * b + lo:C * b + lo + n], ("P%d" % t, C * b + lo, C * b + lo + n)
            gather(P, win, offs(l1, i, lo, n), [(l1, i, i + 1), key], [k], n)
            tt(T["z%d" % t][:, 4 * lo + b:4 * (lo + n):4], win.indirect(offs(l2, i, lo, n)), P, ADD, [(l2, i, i + 1), key, k],
               [("z%d.%d" % (t, b), lo, lo + n)], 0.05 + n * GATHER * CY)
        quant("zq%d" % t, "zs%d" % t, lo, lo + n, "z%d" % t, 4 * lo, 4 * (lo + n), [("z%d.%d" % (t, b), lo, lo + n) for b in range(4)])

    def relu(t, b, lo, n, m):
        out = T["h%d" % t][:, 4 * lo + b:4 * (lo + n):4]
        op("vs", lambda e, q: e.activation(out, m["view"](), ACT.Relu, scale=0.015625) if q == "s" else
           e.tensor_scalar(out, m["view"](), 0.0, 0.015625, MAX, MUL), m["key"], [("h%d.%d" % (t, b), lo, lo + n)], el(n))

    def layer(t, lo, n):
        for b in range(4):
            relu(t, b, lo, n, mm("wq", "wsc", 128 * b, "zq%d" % t, "zs%d" % t, lo, lo + n))
        quant("hq%d" % t, "hs%d" % t, lo, lo + n, "h%d" % t, 4 * lo, 4 * (lo + n), [("h%d.%d" % (t, b), lo, lo + n) for b in range(4)])

    def unpack(t, at, qn, sn, lo, n):
        for b in range(4):
            m, a = mm("eq", "es", 128 * b, qn, sn, lo, lo + n), WIN * b + at
            copy(lambda a=a: T["win%d" % t][:, a:a + n], m["view"], m["key"], [("win%d" % t, a, a + n)], n)

    def exchange(t):
        dest = T.cores[rank ^ (1 << t)]
        rel = relays_of(core, dest, topo)
        en = hop_engines(core, rel, topo)
        ids = [topo.addr(k, core) for k in rel]
        hq, hs, rc, rs = T["hq%d" % t], T["hs%d" % t], T["rc%d" % t], T["rs%d" % t]
        h = G // 2

        def f(e, q):
            e.remote_dma_fused([RemoteDMATransfer(dst_ids=[DstId(rid=ids[k][0], pnc=ids[k][1])], dma_engine_mask=mask_of(en[k]), remote_sem=T.sem["rarr%d" % t],
                                                  src=hq[:, h * k:h * k + h].bitcast(dt.uint8), dst=rc[:, :].bitcast(dt.uint8)) for k in range(2)], local_sem=T.sem["sent"])
            return e.remote_dma(rs[:, :], hs[:, 0:G], T.sem["rarr%d" % t], T.sem["sent"], ids[2][1], ids[2][0], mask_of(en[2]))
        i = op("g", f, [("hq%d" % t, 0, G)], (), 0.6)
        op(None, None, (), full("gq%d" % t), 0.0, sem="garr%d" % t, val=sum(len(topo.engines(k, core)) for k in relays_of(dest, core, topo)),
           lat=HOPS + (FIRST if t == 0 else 0.0), after=[i])
        return sum(len(x) for x in en)

    def scan(dst, src, a, r, cc="cc", n=C):
        op("v", lambda e, q: e.tensor_tensor_scan(T[dst][:], T[cc][:], T[src][:, a:a + C], 0.0, ADD, MAX), r + full(cc), full(dst), el(n))

    def nxrow(t):
        return (0, C) if t == 0 else (WIN + C * (t - 1), WIN + C * t)

    def swap_links(t):
        a, nt = slice(24 * t, 24 * t + 24), slice(24 * t + 24, 24 * t + 48)
        tiny = el(24)

        def me(*names):
            return [(n, t, t + 1) for n in names]

        def nxt(*names):
            return [(n, t + 1, t + 2) for n in names]
        df = ("df", WIN * t, WIN * t + WIN)
        gather(T.dnr[:], T.df[:, df[1]:df[2]], T.pvo[:, a], me("pvo") + [df], full("dnr"), C)
        scan("scd", "dnr", 0, full("dnr"))
        minus(T.dn[:, a], T.scd[:, 15:C:16], "kq", "nkq", full("scd"), me("dn"))
        times(T.dk[:, a], T.dn[:, a], "kk", me("dn"), me("dk"))
        tt(T.db[:, a], T.pf[:, a], T.dk[:, a], SUB, me("pf", "dk"), me("db"), tiny)
        for lo, n in ((0, H), (H, C - H)):
            m = mm("uq16", "us16", 0, "zq%d" % t, "zs%d" % t, lo, lo + n)
            op("v", lambda e, q, m=m, lo=lo, n=n: e.tensor_tensor(T.T1[:, lo:lo + n], m["view"](), T.D[:, C * t + lo:C * t + lo + n], MUL),
               m["key"] + me("D"), [("T1", lo, lo + n)], el(n))
            copy(lambda lo=lo, n=n: T.NT1[:, lo:lo + n], lambda lo=lo, n=n: T.T1[:, lo:lo + n], [("T1", lo, lo + n)], [("NT1", lo, lo + n)], n, scale=-1.0)
        tt(T.sw[:, 0:C], T.T1[:].indirect(T.pro[:, a]), T.NT1[:], LT, full("T1", "NT1", "pro"), [("sw", 0, C)], 0.05 + C * GATHER * CY)
        gather(T.swp[:], T.sw[:], T.pvo[:, a], me("pvo") + [("sw", 0, WIN)], full("swp"), C)
        scan("scq", "swp", 0, full("swp"), "ccb", C // 2)
        tt(T.pa[:, a], T.scq[:, 15:C:16], T.dn[:, a], MUL, full("scq") + me("dn"), me("pa"), tiny)
        tt(T.pf[:, nt], T.pa[:, a], T.db[:, a], ADD, me("pa", "db"), nxt("pf"), tiny)
        copy(lambda: T.pvo[:, nt], lambda: T.pf[:, nt], nxt("pf"), nxt("pvo"), 24, "v")
        scan("scs", "sw", 0, [("sw", 0, C)], "ccb", C // 2)
        tt(T.ta[:, a], T.scs[:, 15:C:16], T.dpr[:, a], MUL, full("scs", "dpr"), me("ta"), tiny)
        tt(T.tb[:, a], T.ta[:, a], T.base[:, a], ADD, me("ta") + full("base"), me("tb"), tiny)
        copy(lambda: T.so[:, a], lambda: T.tb[:, a], me("tb"), me("so"), 24, "v")
        (u, v), (c, d) = nxrow(t), nxrow(t + 1)
        gather(T.nxr[:, c:d], T.nxr[:, u:v], T.so[:, a], me("so") + [("nxr", u, v)], [("nxr", c, d)], C)
        scan("scn", "nxr", c, [("nxr", c, d)])
        ts(T.nxl[:, nt], T.scn[:, 15:C:16], T.kq[:, 0:1], None, SUB, None, full("scn", "kq"), nxt("nxl"))

    for out, src, key, lat in (
            (T.nxi[:], T.nx[:], full("nxi"), 2.1), (T.xw[:, 0:4 * C], T.x[:], [("xw", 0, 4 * C)], 3.8), (T.xw[:, 4 * C:4 * WIN], T.gh[:], [("xw", 4 * C, 4 * WIN)], 4.8),
            (T.pri[:], T.pr[:], full("pri"), 5.2), (T.wq[:].bitcast(dt.uint8), T.wc[:], full("wq"), 6.5), (T.wsc[:], T.ws[:], full("wsc.load"), 7.0),
            (T.ut[:], T.u[:], full("ut"), 7.8), (T.vt[:], T.v[:], full("vt"), 8.6)):
        move(out, src, (), key, lat)

    iota(T.pi[:], [[0, 1]], 0, 1, full("pi"), 1, small=False)
    iota(T.jm[:], [[0, C // 16], [2 * KILL, 16]], 0, 0, full("jm"), C)
    iota(T.t4[:], [[1, 4]], 0, 0, full("t4"), 4)
    op("v", lambda e, q: e.memset(T.half[:], 0.5), (), full("half"), el(WIN))
    op("v", lambda e, q: e.tensor_tensor_scan(T.J[:], T.half[:], T.half[:], -1.0, ADD, ADD), full("half"), full("J"), el(WIN))
    iota(T.jo[:], [[0, R], [16, 24]], 0, 0, full("jo"), 72)
    iota(T.uo[:], [[16, 8]], 0, 0, full("uo"), 8, small=False)
    iota(T.J2[:], [[1, C]], 0, 0, full("J2"), C)
    iota(T.sw[:, C:WIN], [[0, G]], 0, 0, [("sw", C, WIN)], G)
    for k in range(R):
        iota(T.df[:, WIN * k + C:WIN * k + WIN], [[0, G]], 0, 0, [("df", WIN * k + C, WIN * k + WIN)], G)
    ts(T.qi[:], T.pi[:], 15, None, AND, None, full("pi"), full("qi"))
    copy(lambda: T.qf[:], lambda: T.qi[:], full("qi"), full("qf"), 1, "v")
    ts(T.kq[:], T.qf[:], -float(STEP), 15.0 * STEP, MUL, ADD, full("qf"), full("kq"))
    ts(T.kk[:], T.qf[:], -2.0, 30.0, MUL, ADD, full("qf"), full("kk"))
    ts(T.kq4[:], T.t4[:], -0.25, T.kq[:, 0:1], MUL, ADD, full("t4", "kq"), full("kq4"))
    ts(T.nkq[:], T.kq[:], -1.0, None, MUL, None, full("kq"), full("nkq"))
    ts(T.qk[:], T.qf[:], 2.0 * KILL, float(KILL), MUL, ADD, full("qf"), full("qk"))
    ts(T.cc[:], T.jm[:], T.qk[:, 0:1], float(STEP), SUB, MIN, full("jm", "qk"), full("cc"), C)
    copy(lambda: T.ccb[:], lambda: T.cc[:], full("cc"), full("ccb"), C, "s", 2.0 / STEP)
    ts(T.e4[:], T.pi[:], -4.0, -4.0, MUL, ADD, full("pi"), full("e4"))
    op("s", lambda e, q: e.activation(T.ab[:], T.J[:, 0:528], ACT.Abs, bias=T.e4[:, 0:1]), full("J", "e4"), full("ab"), el(528))
    op("s", lambda e, q: e.activation(T.ee[:], T.ab[:], ACT.Relu, bias=1.0, scale=-1.0), full("ab"), full("ee"), el(528))
    for b in range(4):
        quant("eq", "es", 128 * b, 128 * b + 128, "ee", 4 - b, 516 - b, full("ee"))

    copy(lambda: T.nxo[:], lambda: T.nxi[:], full("nxi"), full("nxo"), 36, "v")
    for b in range(4):
        ts(T.nx4[:, 24 * b:24 * b + 24], T.nxi[:, 0:24], 4.0, float(b), MUL, ADD, full("nxi"), [("nx4", b, b + 1)])
    op("v", lambda e, q: e.tensor_copy(T.pvr[:].indirect(T.nxo[:]), T.J[:]), full("J", "nxo"), full("pvr"), 0.05 + WIN * SCATTER * CY)
    gather(T.nxr[:, 0:WIN], T.J[:], T.nxo[:], full("J", "nxo"), [("nxr", 0, WIN)], WIN, "s")
    scan("scp", "pvr", 0, full("pvr"))
    for b in range(4):
        ts(T.pv4[:, 24 * b:24 * b + 24], T.scp[:, 15:C:16], T.kq4[:, b:b + 1], 4.0, SUB, MUL, full("scp", "kq4"), [("pv4", b, b + 1)])
    ts(T.pvo[:, 0:24], T.scp[:, 15:C:16], T.kq[:, 0:1], None, SUB, None, full("scp", "kq"), [("pvo", 0, 1)])
    minus(T.pf[:, 0:24], T.scp[:, 15:C:16], "kq", "nkq", full("scp"), [("pf", 0, 1)])
    copy(lambda: T.pro[:], lambda: T.pri[:], full("pri"), full("pro"), 72, "v")
    copy(lambda: T.prf[:], lambda: T.pri[:], full("pri"), full("prf"), 72, "v")
    ts(T.joq[:], T.jo[:], T.qf[:, 0:1], None, ADD, None, full("jo", "qf"), full("joq"), 72)
    tt(T.dpr[:], T.prf[:], T.joq[:], SUB, full("prf", "joq"), full("dpr"), el(144))
    times(T.kd[:], T.dpr[:], "kk", full("dpr"), full("kd"), 72)
    tt(T.base[:], T.joq[:], T.kd[:], SUB, full("joq", "kd"), full("base"), el(144))
    for i in range(R):
        d, key = T.df[:, WIN * i:WIN * i + C], [("df", WIN * i, WIN * i + C)]
        tt(d, T.J[:, 0:C].indirect(T.pro[:, 24 * i:24 * i + 24]), T.J2[:], SUB, full("J", "J2", "pro"), key, 0.05 + C * GATHER * CY)
        op("s", lambda e, q, i=i, d=d: e.activation(T.D[:, C * i:C * i + C], d, ACT.Sign), key, [("D", i, i + 1)], el(C))
    quant("uq", "us", 0, 128, "ut", 0, 512, full("ut"))
    copy(lambda: T.uof[:], lambda: T.uo[:], full("uo"), full("uof"), 8, "v")
    op("v", lambda e, q: e.tensor_copy(T.uq16[:, 0:128].bitcast(dt.uint32), T.uq[:, 0:128].bitcast(dt.uint32).indirect(T.uof[:, 0:8])),
       full("uq", "uof"), full("uq16"), 0.05 + 128 * GATHER * CY)
    gather(T.us16[:, 0:128], T.us[:, 0:128], T.uof[:, 0:8], full("uq", "uof"), full("us16.load"), 128)
    quant("vq", "vs", 0, 128, "vt", 0, 512, full("vt"))

    sent = 0
    for t in range(R):
        read(t, 0, H)
        layer(t, 0, H)
        sent += exchange(t)
        read(t, H, C - H)
        swap_links(t)
        layer(t, H, C - H)
        unpack(t + 1, 0, "hq%d" % t, "hs%d" % t, 0, H)
        unpack(t + 1, H, "hq%d" % t, "hs%d" % t, H, C - H)
        unpack(t + 1, C, "gq%d" % t, "gs%d" % t, 0, G)
    c, d = nxrow(R)
    move(T.nl[:, C:WIN], T.nxr[0:128:16, C:WIN], [("nxr", C, WIN)], [("nl", C, WIN)])
    move(T.nl[:, 0:C], T.nxr[0:128:16, c:d], [("nxr", c, d)], [("nl", 0, C)])
    zq, zs, qn = T["zq%d" % R], T["zs%d" % R], "zq%d" % R
    for lo, n in ((0, 256), (256, 128)):
        read(R, lo, n)
        m = mm("vq", "vs", 0, qn, "zs%d" % R, lo, lo + n)
        move(T.oc[:, 4 * lo:4 * (lo + n)], zq[:, lo:lo + n].bitcast(dt.uint8), [(qn, lo, lo + n)], [("oc", lo, lo + n)], 2.3)
        copy(lambda lo=lo, n=n: T.y_sb[:, lo:lo + n], m["view"], m["key"], [("y_sb", lo, lo + n)], n)
        move(T.y[:, lo:lo + n], T.y_sb[:, lo:lo + n], [("y_sb", lo, lo + n)], [("y", lo, lo + n)], 2.3)
    for k in range(4):
        move(T.osc[4 * k:4 * k + 4, :], zs[32 * k:32 * k + 4, :], [(qn, 0, C)], [("osc", k, k + 1)], q="s")
    op("y", None, [("oc", 0, C), ("y", 0, C), ("osc", 0, 4), ("nl", 0, WIN)], (), 0.0)
    emit(g, T, arrange(ops))
    g.wait_ge(T.sem.sent, sent)
